import numpy as np
import ml_dtypes


def mxq(x, axis, fmt="e4m3"):
    dtype, down = {"e4m3": (ml_dtypes.float8_e4m3fn, 7), "e5m2": (ml_dtypes.float8_e5m2, 14)}[fmt]
    v = np.moveaxis(np.asarray(x, np.float32).astype(ml_dtypes.bfloat16).astype(np.float64), axis, -1)
    blocks = v.reshape(v.shape[:-1] + (-1, 32))
    amax = np.abs(blocks).max(-1, keepdims=True)
    byte = np.maximum(np.where(amax > 0, np.frexp(amax)[1] - 1 + 127, 0) - down, 1)
    scale = np.exp2(byte - 127.0)
    codes = (blocks / scale).astype(np.float32).astype(dtype).astype(np.float64)
    return np.moveaxis((codes * scale).reshape(v.shape), -1, axis)


WIDE = False


def mx_kscale(k):
    if not WIDE:
        return np.ones(k)
    levels = np.array([10, -10, 5, -5, 0])
    if k % 512:
        return np.exp2(np.random.permutation(np.resize(levels, k // 32))).repeat(32)
    a = np.empty((k // 512, 16))
    for p in range(k // 512):
        a[p, :8] = np.random.permutation(np.resize(levels, 8))
        for g in range(8):
            far = levels[np.abs(levels - a[p, g]) >= 10]
            a[p, g + 8] = far[np.random.randint(len(far))]
    return np.exp2(a.ravel()).repeat(32)


BF16 = ml_dtypes.bfloat16


def bf(x):
    return np.asarray(x, np.float32).astype(BF16)


def f64(x):
    return np.asarray(x).astype(np.float64)


E2M1 = np.array([0.0, 0.5, 1.0, 1.5, 2.0, 3.0, 4.0, 6.0, -0.0, -0.5, -1.0, -1.5, -2.0, -3.0, -4.0, -6.0])


def pack_weight(w, fmt):
    k, n = w.shape
    w = f64(bf(w)).reshape(k // 32, 32, n)
    amax = np.abs(w).max(1)
    if fmt == "e4m3":
        byte = np.frexp(amax)[1] - 1 + 127 - 7
    else:
        mant, ex = np.frexp(amax / 6.0)
        byte = np.where(mant > 0.5, ex, ex - 1) + 127
    byte = np.clip(np.where(amax > 0, byte, 1), 1, 254)
    scaled = (w * np.exp2(127.0 - byte)[:, None, :]).reshape(k, n).astype(np.float32)
    by_word = np.ascontiguousarray(scaled.reshape(k // 512, 128, 4, n).transpose(0, 1, 3, 2))
    if fmt == "e4m3":
        words = by_word.astype(ml_dtypes.float8_e4m3fn).view(np.uint8)
    else:
        c = by_word.astype(ml_dtypes.float4_e2m1fn).view(np.uint8) & 0xF
        words = c[..., 0::2] | (c[..., 1::2] << 4)
    return np.ascontiguousarray(words), np.ascontiguousarray(byte.astype(np.uint8).reshape(k // 512, 16, n))


def unpack_weight(words, scales, fmt):
    g, p, n, _ = words.shape
    if fmt == "e4m3":
        vals = np.ascontiguousarray(words).view(ml_dtypes.float8_e4m3fn).astype(np.float64)
    else:
        nib = np.empty((g, p, n, 4), np.uint8)
        nib[..., 0::2] = words & 0xF
        nib[..., 1::2] = words >> 4
        vals = E2M1[nib]
    vals = vals * np.repeat(np.exp2(scales.astype(np.float64) - 127.0), 8, axis=1)[..., None]
    return vals.transpose(0, 1, 3, 2).reshape(g * 512, n)

def planes(Y):
    n, m = Y.shape
    b = f64(bf(Y)).reshape(n // 32, 32, m)
    amax = np.abs(b).max(1)
    byte = np.clip(np.where(amax > 0, np.frexp(amax)[1] - 1 + 127 - 7, 1), 1, 254)
    codes = (b * np.exp2(127.0 - byte)[:, None, :]).reshape(n, m).astype(np.float32).astype(ml_dtypes.float8_e4m3fn).view(np.uint8)
    words = codes.reshape(n // 512, 128, 4, m).transpose(0, 1, 3, 2)
    return np.ascontiguousarray(words), np.ascontiguousarray(byte.astype(np.uint8).reshape(n // 512, 16, m))


D, F, N = 1024, 1024, 512

ALPHA = 0.5


def setup_inputs():
    s = mx_kscale(N)
    t = mx_kscale(N)
    c = 1.0 / np.sqrt(N)
    w0 = bf(np.random.standard_normal((D, F)) * 0.5)
    coef_words, coef_scales = pack_weight((np.random.standard_normal((N, N)) * c * s[None, :]).T, "e4m3")
    g = bf((1.0 + 0.1 * np.random.standard_normal(N)) * t)
    uc_words, uc_scales = pack_weight((np.random.standard_normal((D, N)) * c / t[None, :]).T, "e4m3")
    us_words, us_scales = pack_weight((np.random.standard_normal((D, N)) * c / t[None, :]).T, "e4m3")
    vc_words, vc_scales = pack_weight(np.random.standard_normal((N, F)) / s[:, None], "e4m3")
    vs_words, vs_scales = pack_weight(np.random.standard_normal((N, F)) / s[:, None], "e4m3")
    return {
        "w0": w0,
        "coef_words": coef_words,
        "coef_scales": coef_scales,
        "g": g,
        "uc_words": uc_words,
        "uc_scales": uc_scales,
        "us_words": us_words,
        "us_scales": us_scales,
        "vc_words": vc_words,
        "vc_scales": vc_scales,
        "vs_words": vs_words,
        "vs_scales": vs_scales,
    }


def core(w0, coef_words, coef_scales, g, uc_words, uc_scales, us_words, us_scales, vc_words, vc_scales, vs_words, vs_scales):
    cq = unpack_weight(coef_words, coef_scales, "e4m3").T
    rc = cq @ unpack_weight(vc_words, vc_scales, "e4m3")
    rs = cq @ unpack_weight(vs_words, vs_scales, "e4m3")
    gain = f64(g)[:, None]
    zc = gain * rc
    zs = gain * rs
    pc = unpack_weight(uc_words, uc_scales, "e4m3").T @ mxq(zc, 0, "e4m3")
    ps = unpack_weight(us_words, us_scales, "e4m3").T @ mxq(zs, 0, "e4m3")
    return f64(w0) + ALPHA * (pc - ps)


def reference(w0, coef_words, coef_scales, g, uc_words, uc_scales, us_words, us_scales, vc_words, vc_scales, vs_words, vs_scales):
    R_out = core(w0, coef_words, coef_scales, g, uc_words, uc_scales, us_words, us_scales, vc_words, vc_scales, vs_words, vs_scales)
    words, scales = planes(R_out)
    return R_out, words, scales

@@ -1,0 +1,230 @@
+from contextlib import ExitStack
+
+import concourse.mybir as mybir
+
+D, F, N = 1024, 1024, 512
+FLOPS = 2 * (2 * N * N * F) + 2 * (2 * D * N * F)
+F32 = mybir.dt.float32
+BF16 = mybir.dt.bfloat16
+I32 = mybir.dt.int32
+U32 = mybir.dt.uint32
+U8 = mybir.dt.uint8
+FP8X4 = mybir.dt.float8_e4m3fn_x4
+ALU = mybir.AluOpType
+ACT = mybir.ActivationFunctionType
+P = 128
+CFG = {'q': {'cs': ['S', 'S', 'S', 'S'], 'vcs': ['S', 'S', 'SP', 'SP'], 'vss': ['SP', 'SP', 'SP', 'SP'], 'ucs': ['SP', 'SP', 'SP', 'SP'], 'uss': ['SP', 'SP', 'SP', 'SP'], 'g': 'SP'}, 'vload': [[0, 512], [512, 512]], 'wload': [[0, 512], [512, 512]], 'z': [[0, 256], [256, 256], [512, 256], [768, 256]], 'amode': [['V', 'V'], ['SV', 'SV'], ['SS', 'SV'], ['SS', 'SS']], 'units': [[0, 0, 256, 'S'], [1, 0, 256, 'S'], [0, 256, 256, 'S'], [1, 256, 256, 'S'], [0, 512, 256, 'S'], [1, 512, 256, 'S'], [0, 768, 256, 'S'], [1, 768, 128, 'S'], [1, 896, 128, 'S']], 'wstore': [[0, 1], [2, 3], [4, 5], [6], [7, 8]], 'wq': ['SP', 'SP', 'SP', 'SP', 'S'], 'sstore': [[0, 1, 2, 3], [4, 5, 6, 7, 8]], 'sq': [['G', 'G', 'G', 'G'], ['S', 'SP', 'S', 'SP']], 'uwhole': False, 'bigq': {'uc0': 'G', 'us0': 'G', 'vc1': 'G', 'vs1': 'G', 'uc1': 'G', 'us1': 'G'}, 'iz': 4, 'id': 2, 'oq': ['SP', 'SP', 'SP', 'SP', 'SP', 'SP', 'SP', 'SP', 'SP']}
+ORDER = ['ms_a', 'warm', 'L_coef', 'L_uc0', 'L_vc0', 'ms_b', 'L_cs0', 'L_cs1', 'L_cs2', 'L_us0', 'L_cs3', 'L_vcs0', 'L_vcs1', 'L_vc1', 'L_uc1', 'F_cw', 'L_vcs2', 'L_vcs3', 'L_g', 'L_vs0', 'F_cs', 'L_vss0', 'L_us1', 'L_vss1', 'L_vss2', 'L_vss3', 'L_vs1', 'F_uc0', 'L_ucs0', 'M1_0c0', 'L_ucs1', 'gain', 'L_ucs2', 'M1_1c1', 'L_ucs3', 'L_uss0', 'A_0c0', 'L_uss1', 'L_uss2', 'L_uss3', 'M1_1c0', 'A_1c1', 'L_w0_0', 'M1_0s1', 'L_w1_0', 'F_us0', 'L_w0_1', 'A_1c0', 'M1_1s1', 'L_w1_1', 'A_0s1', 'M1_1s0', 'A_1s1', 'M1_0s0', 'I_1c', 'M1_0c1', 'A_1s0', 'M1_3c1', 'A_0s0', 'M1_2c1', 'A_3c1', 'M1_3s0', 'F_uc1', 'M1_2s0', 'B_0s', 'A_3s0', 'M1_2s1', 'A_0c1', 'M1_3s1', 'M1_3c0', 'A_2s0', 'B_1c', 'M1_2c0', 'F_us_0', 'A_2c1', 'B_0c', 'I_1s', 'A_2s1', 'M2_0_1', 'F_us1', 'A_2c0', 'M2_0_0', 'F_us_1', 'B_1s', 'A_3s1', 'M2_1_0', 'I_2s', 'A_3c0', 'M2_1_1', 'C_0_0', 'I_2c', 'M2_2_0', 'C_0_1', 'M2_2_1', 'B_2s', 'S_o0', 'C_1_1', 'M2_3_1', 'D_0', 'C_1_0', 'M2_3_0', 'B_2c', 'S_o1', 'I_3c', 'C_2_1', 'M2_5_1', 'C_2_0', 'M2_4_0', 'I_3s', 'C_3_1', 'S_o2', 'M2_5_0', 'C_3_0', 'M2_4_1', 'C_4_0', 'D_2', 'S_o3', 'C_4_1', 'B_3c', 'D_3', 'S_o4', 'C_5_0', 'C_5_1', 'D_1', 'B_3s', 'S_o5', 'E_2', 'M2_7_0', 'E_3', 'E_0', 'S_w1', 'M2_8_0', 'D_5', 'E_1', 'C_7_0', 'M2_6_1', 'S_s0_0', 'S_w0', 'C_8_0', 'M2_6_0', 'D_4', 'S_s0_3', 'C_6_1', 'S_o8', 'S_o7', 'S_s0_2', 'C_6_0', 'D_8', 'E_5', 'S_s0_1', 'S_o6', 'D_6', 'E_8', 'E_4', 'S_w2', 'D_7', 'E_6', 'S_w3', 'E_7', 'S_w4', 'S_s1_3', 'S_s1_2', 'S_s1_1', 'S_s1_0']
+
+
+def tile_fourierftgivenbases_x2_kernel(tc, w0, coef_words, coef_scales, g, uc_words, uc_scales,
+                                                  us_words, us_scales, vc_words, vc_scales, vs_words, vs_scales,
+                                                  out_0, out_1, out_2):
+    nc = tc.nc
+    queue = {"SP": nc.sync, "S": nc.scalar, "G": nc.gpsimd}
+    with ExitStack() as ctx:
+        keep = ctx.enter_context(tc.tile_pool(name="keep", bufs=1))
+        psum = ctx.enter_context(tc.psum_pool(name="psum", bufs=1))
+        ctx.enter_context(tc.manual_schedule())
+
+        def sb(name, shape, dtype):
+            return keep.tile(shape, dtype, name=name, align_bytes=256)
+
+        planes_a = sb("planes_a", [P, N + F], U8)
+        planes_b = sb("planes_b", [P, F + D], U8)
+        raw_plane = {"cs": planes_a[:, 0:N], "vcs": planes_a[:, N:], "vss": planes_b[:, 0:F],
+                     "ucs": planes_b[:, F:], "uss": planes_b[:, F:]}
+        plane_row = {"cs": 0, "vcs": 0, "vss": 0, "ucs": 0, "uss": 4}
+        plane_src = {"cs": coef_scales, "vcs": vc_scales, "vss": vs_scales, "ucs": uc_scales, "uss": us_scales}
+        coef_raw = sb("coef_raw", [P, N], U32)
+        coef_w = sb("coef_w", [P, N], U32)
+        coef_s = sb("coef_s", [P, N], U8)
+        u_raw = {b: sb("u_raw" + b, [P, D], U32) for b in "cs"}
+        u_w = {b: sb("u_w" + b, [P, D], U32) for b in "cs"}
+        u_s = sb("u_s", [P, D], U8)
+        v_w = {b: sb("v_w" + b, [P, F], U32) for b in "cs"}
+        u_src = {"c": uc_words, "s": us_words}
+        v_src = {"c": vc_words, "s": vs_words}
+        g_sb = sb("g_sb", [P, 4], BF16)
+        gains = sb("gains", [P, 2, 4], F32)
+        warm = sb("warm", [P, 2], F32)
+        w_sb = {(G, i): sb("w_sb%d_%d" % (G, i), [P, 4, w], BF16) for G in range(2) for i, (f0, w) in enumerate(CFG["wload"])}
+        z_t = {(j, b): sb("z_t%d%s" % (j, b), [P, 4, w], BF16) for j, (f0, w) in enumerate(CFG["z"]) for b in "cs"
+               if CFG["amode"][j]["cs".index(b)] != "V"}
+        z_i = {(j, b): sb("z_i%d%s" % (j, b), [P, w, 4], BF16) for j, (f0, w) in enumerate(CFG["z"]) for b in "cs"}
+        z_w = {(j, b): sb("z_w%d%s" % (j, b), [P, w], U32) for j, (f0, w) in enumerate(CFG["z"]) for b in "cs"}
+        z_s = {(j, b): sb("z_s%d%s" % (j, b), [P, w], U8) for j, (f0, w) in enumerate(CFG["z"]) for b in "cs"}
+        res = [sb("res%d" % u, [P, 4, un[2]], F32) for u, un in enumerate(CFG["units"])]
+        res_i = [sb("res_i%d" % u, [P, un[2], 4], BF16) for u, un in enumerate(CFG["units"])]
+        out_w = sb("out_w", [P, 2, F], U32)
+        out_s = sb("out_s", [P, 2, F], U8)
+        banks = {}
+        count = []
+
+        def new_bank(key):
+            bank = psum.tile([P, 512], F32, name="bank%d" % (len(count) % 8))
+            count.append(key)
+            banks[key] = bank
+            return bank
+
+        def find(ranges, f):
+            return [i for i, r in enumerate(ranges) if r[0] <= f < r[0] + r[1]][0]
+
+        def words(ap, c0, c1):
+            return ap[0].rearrange("p n t -> p (n t)")[:, 4 * c0:4 * c1].bitcast(I32)
+
+        def permute(dst, src):
+            nc.vector.tensor_copy(out=dst.rearrange("p (t m) -> p m t", t=4), in_=src.rearrange("p (m t) -> p m t", t=4))
+
+        def bigq(n):
+            return queue[CFG["bigq"].get(n, "SP")]
+
+        for step in ORDER:
+            part = step.split("_")
+            kind = part[0]
+            if step == "ms_a":
+                nc.vector.memset(planes_a[:].bitcast(I32), 0)
+            elif step == "ms_b":
+                nc.vector.memset(planes_b[:].bitcast(I32), 0)
+            elif step == "warm":
+                nc.gpsimd.memset(warm[:, 0:1], 0.0)
+                nc.scalar.activation(out=warm[:, 1:2], in_=warm[:, 0:1], func=ACT.Copy)
+            elif step == "gain":
+                nc.scalar.activation(out=gains[:, 0, :], in_=g_sb[:], func=ACT.Copy)
+                nc.scalar.activation(out=gains[:, 1, :], in_=g_sb[:], func=ACT.Copy, scale=-1.0)
+            elif step == "L_coef":
+                nc.sync.dma_start(out=coef_raw[:].bitcast(I32), in_=words(coef_words, 0, N))
+            elif step == "L_g":
+                queue[CFG["q"]["g"]].dma_start(out=g_sb[:], in_=g.rearrange("(p t) -> p t", t=4))
+            elif kind == "L" and part[1][:-1] in raw_plane:
+                name, Q = part[1][:-1], int(part[1][-1])
+                q = CFG["q"][name]
+                r = 32 * Q + plane_row[name]
+                queue[q[Q]].dma_start(
+                    out=raw_plane[name][r:r + 4, :].bitcast(I32), in_=plane_src[name][0, 4 * Q:4 * Q + 4, :].bitcast(I32))
+            elif kind == "L" and part[1][0] == "u":
+                b, G = part[1][1], int(part[1][2])
+                c0, c1 = (0, D) if CFG["uwhole"] else (512 * G, 512 * G + 512)
+                bigq(part[1]).dma_start(out=u_raw[b][:, c0:c1].bitcast(I32), in_=words(u_src[b], c0, c1))
+            elif kind == "L" and part[1][0] == "v":
+                b, i = part[1][1], int(part[1][2])
+                f0, w = CFG["vload"][i]
+                bigq(part[1]).dma_start(out=v_w[b][:, f0:f0 + w].bitcast(I32), in_=words(v_src[b], f0, f0 + w))
+            elif kind == "L":
+                G, i = int(part[1][1]), int(part[2])
+                f0, w = CFG["wload"][i]
+                bigq("w%d_%d" % (G, i)).dma_start(
+                    out=w_sb[(G, i)][:], in_=w0[512 * G:512 * G + 512, f0:f0 + w].rearrange("(p t) f -> p t f", t=4))
+            elif step == "F_cw":
+                permute(coef_w[:].bitcast(I32), coef_raw[:].bitcast(I32))
+            elif step == "F_cs":
+                permute(coef_s[:], raw_plane["cs"])
+            elif kind == "F" and len(part) == 3:
+                G = int(part[2])
+                permute(u_s[:, 512 * G:512 * G + 512], raw_plane["ucs"][:, 512 * G:512 * G + 512])
+            elif kind == "F":
+                b, G = part[1][1], int(part[1][2])
+                permute(u_w[b][:, 512 * G:512 * G + 512].bitcast(I32), u_raw[b][:, 512 * G:512 * G + 512].bitcast(I32))
+            elif kind in ("M1", "A"):
+                j, b, k = int(part[1][0]), part[1][1], int(part[1][2])
+                f0, w = CFG["z"][j]
+                direct = CFG["amode"][j]["cs".index(b)] == "V"
+                if direct:
+                    n, per, ts, c0 = 128, 4, range(4), f0 + 128 * k
+                else:
+                    per = 512 // w
+                    n, ts, c0 = w, range(per * k, per * k + per), f0
+                if kind == "M1":
+                    bank = new_bank((1, j, b, k))
+                    for i, t in enumerate(ts):
+                        nc.tensor.matmul_mx(
+                            out=bank[:, i * n:(i + 1) * n],
+                            lhsT=coef_w[:, 128 * t:128 * t + 128].bitcast(FP8X4), lhsT_scale=coef_s[:, 128 * t:128 * t + 128],
+                            rhs=v_w[b][:, c0:c0 + n].bitcast(FP8X4), rhs_scale=raw_plane["v" + b + "s"][:, c0:c0 + n],
+                            start=True, stop=True)
+                elif direct:
+                    bi = "cs".index(b)
+                    nc.vector.tensor_tensor(
+                        out=z_i[(j, b)][:, 128 * k:128 * k + 128, :],
+                        in0=banks[(1, j, b, k)][:].rearrange("p (t n) -> p n t", t=4),
+                        in1=gains[:, bi:bi + 1, :].broadcast_to([P, 128, 4]), op=ALU.mult)
+                else:
+                    for i, t in enumerate(ts):
+                        nc.scalar.activation(out=z_t[(j, b)][:, t, :], in_=banks[(1, j, b, k)][:, i * n:(i + 1) * n],
+                                             func=ACT.Copy, scale=gains[:, "cs".index(b), t:t + 1])
+            elif kind == "I":
+                j, b = int(part[1][0]), part[1][1]
+                mode = CFG["amode"][j]["cs".index(b)]
+                dst = z_i[(j, b)][:].rearrange("p (c i) t -> p c t i", i=CFG["iz"])
+                src = z_t[(j, b)][:].rearrange("p t (c i) -> p c t i", i=CFG["iz"])
+                if mode == "SV":
+                    nc.vector.tensor_copy(out=dst, in_=src)
+                elif mode == "SG":
+                    nc.gpsimd.tensor_scalar(out=dst, in0=src, scalar1=1.0, scalar2=0.0, op0=ALU.mult, op1=ALU.add)
+                else:
+                    nc.scalar.copy(out=dst, in_=src)
+            elif kind == "B":
+                j, b = int(part[1][0]), part[1][1]
+                nc.vector.quantize_mx(out=z_w[(j, b)][:].bitcast(FP8X4), scales=z_s[(j, b)][:],
+                                      in_=z_i[(j, b)][:].rearrange("p n t -> p (n t)"))
+            elif kind in ("M2", "C"):
+                u, k = int(part[1]), int(part[2])
+                G, f0, w, dm = CFG["units"][u]
+                per = 512 // w
+                ts = range(per * k, per * k + per)
+                if kind == "M2":
+                    j = find(CFG["z"], f0)
+                    c0 = f0 - CFG["z"][j][0]
+                    bank = new_bank((2, u, k))
+                    for i, t in enumerate(ts):
+                        m0 = 512 * G + 128 * t
+                        for b in "cs":
+                            nc.tensor.matmul_mx(
+                                out=bank[:, i * w:(i + 1) * w],
+                                lhsT=u_w[b][:, m0:m0 + 128].bitcast(FP8X4),
+                                lhsT_scale=u_s[plane_row["u" + b + "s"]:, m0:m0 + 128],
+                                rhs=z_w[(j, b)][:, c0:c0 + w].bitcast(FP8X4), rhs_scale=z_s[(j, b)][:, c0:c0 + w],
+                                start=(b == "c"), stop=(b == "s"))
+                else:
+                    wi = find(CFG["wload"], f0)
+                    c0 = f0 - CFG["wload"][wi][0]
+                    nc.vector.scalar_tensor_tensor(
+                        out=res[u][:, per * k:per * k + per, :],
+                        in0=banks[(2, u, k)][:].rearrange("p (t n) -> p t n", t=per), scalar=0.5,
+                        in1=w_sb[(G, wi)][:, per * k:per * k + per, c0:c0 + w], op0=ALU.mult, op1=ALU.add)
+            elif kind == "D":
+                u = int(part[1])
+                dst = res_i[u][:].rearrange("p (c i) t -> p c t i", i=CFG["id"])
+                src = res[u][:].rearrange("p t (c i) -> p c t i", i=CFG["id"])
+                if CFG["units"][u][3] == "S":
+                    nc.scalar.copy(out=dst, in_=src)
+                elif CFG["units"][u][3] == "G":
+                    nc.gpsimd.tensor_scalar(out=dst, in0=src, scalar1=1.0, scalar2=0.0, op0=ALU.mult, op1=ALU.add)
+                else:
+                    nc.vector.tensor_copy(out=dst, in_=src)
+            elif kind == "E":
+                u = int(part[1])
+                G, f0, w, dm = CFG["units"][u]
+                nc.vector.quantize_mx(out=out_w[:, G, f0:f0 + w].bitcast(FP8X4), scales=out_s[:, G, f0:f0 + w],
+                                      in_=res_i[u][:].rearrange("p n t -> p (n t)"))
+            elif part[1][0] == "o":
+                u = int(part[1][1:])
+                G, f0, w, dm = CFG["units"][u]
+                queue[CFG["oq"][u]].dma_start(
+                    out=out_0[512 * G:512 * G + 512, f0:f0 + w].rearrange("(p t) f -> p t f", t=4), in_=res[u][:])
+            else:
+                s = int(part[1][1:])
+                us = CFG["wstore" if part[1][0] == "w" else "sstore"][s]
+                Gs = sorted(set(CFG["units"][u][0] for u in us))
+                f0 = min(CFG["units"][u][1] for u in us)
+                f1 = max(CFG["units"][u][1] + CFG["units"][u][2] for u in us)
+                G0, G1 = Gs[0], Gs[-1] + 1
+                if part[1][0] == "w":
+                    queue[CFG["wq"][s]].dma_start(
+                        out=out_1[G0:G1].rearrange("g p f t -> p g (f t)")[:, :, 4 * f0:4 * f1].bitcast(I32),
+                        in_=out_w[:, G0:G1, f0:f1].bitcast(I32))
+                else:
+                    Q = int(part[2])
+                    queue[CFG["sq"][s][Q]].dma_start(
+                        out=out_2[G0:G1, 4 * Q:4 * Q + 4, f0:f1].rearrange("g r f -> r g f").bitcast(I32),
+                        in_=out_s[32 * Q:32 * Q + 4, G0:G1, f0:f1].bitcast(I32))

@@ -13,8 +13,8 @@ FP8X4 = mybir.dt.float8_e4m3fn_x4
 ALU = mybir.AluOpType
 ACT = mybir.ActivationFunctionType
 P = 128
-CFG = {'q': {'cs': ['S', 'S', 'S', 'S'], 'vcs': ['S', 'S', 'SP', 'SP'], 'vss': ['SP', 'SP', 'SP', 'SP'], 'ucs': ['SP', 'SP', 'SP', 'SP'], 'uss': ['SP', 'SP', 'SP', 'SP'], 'g': 'SP'}, 'vload': [[0, 512], [512, 512]], 'wload': [[0, 512], [512, 512]], 'z': [[0, 256], [256, 256], [512, 256], [768, 256]], 'amode': [['V', 'V'], ['SV', 'SV'], ['SS', 'SV'], ['SS', 'SS']], 'units': [[0, 0, 256, 'S'], [1, 0, 256, 'S'], [0, 256, 256, 'S'], [1, 256, 256, 'S'], [0, 512, 256, 'S'], [1, 512, 256, 'S'], [0, 768, 256, 'S'], [1, 768, 128, 'S'], [1, 896, 128, 'S']], 'wstore': [[0, 1], [2, 3], [4, 5], [6], [7, 8]], 'wq': ['SP', 'SP', 'SP', 'SP', 'S'], 'sstore': [[0, 1, 2, 3], [4, 5, 6, 7, 8]], 'sq': [['G', 'G', 'G', 'G'], ['S', 'SP', 'S', 'SP']], 'uwhole': False, 'bigq': {'uc0': 'G', 'us0': 'G', 'vc1': 'G', 'vs1': 'G', 'uc1': 'G', 'us1': 'G'}, 'iz': 4, 'id': 2, 'oq': ['SP', 'SP', 'SP', 'SP', 'SP', 'SP', 'SP', 'SP', 'SP']}
-ORDER = ['ms_a', 'warm', 'L_coef', 'L_uc0', 'L_vc0', 'ms_b', 'L_cs0', 'L_cs1', 'L_cs2', 'L_us0', 'L_cs3', 'L_vcs0', 'L_vcs1', 'L_vc1', 'L_uc1', 'F_cw', 'L_vcs2', 'L_vcs3', 'L_g', 'L_vs0', 'F_cs', 'L_vss0', 'L_us1', 'L_vss1', 'L_vss2', 'L_vss3', 'L_vs1', 'F_uc0', 'L_ucs0', 'M1_0c0', 'L_ucs1', 'gain', 'L_ucs2', 'M1_1c1', 'L_ucs3', 'L_uss0', 'A_0c0', 'L_uss1', 'L_uss2', 'L_uss3', 'M1_1c0', 'A_1c1', 'L_w0_0', 'M1_0s1', 'L_w1_0', 'F_us0', 'L_w0_1', 'A_1c0', 'M1_1s1', 'L_w1_1', 'A_0s1', 'M1_1s0', 'A_1s1', 'M1_0s0', 'I_1c', 'M1_0c1', 'A_1s0', 'M1_3c1', 'A_0s0', 'M1_2c1', 'A_3c1', 'M1_3s0', 'F_uc1', 'M1_2s0', 'B_0s', 'A_3s0', 'M1_2s1', 'A_0c1', 'M1_3s1', 'M1_3c0', 'A_2s0', 'B_1c', 'M1_2c0', 'F_us_0', 'A_2c1', 'B_0c', 'I_1s', 'A_2s1', 'M2_0_1', 'F_us1', 'A_2c0', 'M2_0_0', 'F_us_1', 'B_1s', 'A_3s1', 'M2_1_0', 'I_2s', 'A_3c0', 'M2_1_1', 'C_0_0', 'I_2c', 'M2_2_0', 'C_0_1', 'M2_2_1', 'B_2s', 'S_o0', 'C_1_1', 'M2_3_1', 'D_0', 'C_1_0', 'M2_3_0', 'B_2c', 'S_o1', 'I_3c', 'C_2_1', 'M2_5_1', 'C_2_0', 'M2_4_0', 'I_3s', 'C_3_1', 'S_o2', 'M2_5_0', 'C_3_0', 'M2_4_1', 'C_4_0', 'D_2', 'S_o3', 'C_4_1', 'B_3c', 'D_3', 'S_o4', 'C_5_0', 'C_5_1', 'D_1', 'B_3s', 'S_o5', 'E_2', 'M2_7_0', 'E_3', 'E_0', 'S_w1', 'M2_8_0', 'D_5', 'E_1', 'C_7_0', 'M2_6_1', 'S_s0_0', 'S_w0', 'C_8_0', 'M2_6_0', 'D_4', 'S_s0_3', 'C_6_1', 'S_o8', 'S_o7', 'S_s0_2', 'C_6_0', 'D_8', 'E_5', 'S_s0_1', 'S_o6', 'D_6', 'E_8', 'E_4', 'S_w2', 'D_7', 'E_6', 'S_w3', 'E_7', 'S_w4', 'S_s1_3', 'S_s1_2', 'S_s1_1', 'S_s1_0']
+CFG = {'q': {'cs': ['SP', 'SP', 'SP', 'SP'], 'vcs': ['SP', 'SP', 'SP', 'SP'], 'vss': ['SP', 'SP', 'SP', 'SP'], 'ucs': ['SP', 'SP', 'SP', 'SP'], 'uss': ['SP', 'SP', 'G', 'G'], 'g': 'G'}, 'vload': [[0, 512], [512, 512]], 'wload': [[0, 512], [512, 512]], 'z': [[0, 256], [256, 256], [512, 256], [768, 256]], 'amode': [['V', 'V'], ['SS', 'V'], ['SS', 'V'], ['SS', 'SS']], 'units': [[0, 0, 256, [['S', 0, 256]]], [1, 0, 256, [['S', 0, 256]]], [0, 256, 256, [['S', 0, 256]]], [1, 256, 256, [['S', 0, 256]]], [0, 512, 256, [['S', 0, 256]]], [1, 512, 256, [['S', 0, 256]]], [0, 768, 256, [['S', 0, 256]]], [1, 768, 128, [['S', 0, 128]]], [1, 896, 128, [['S', 0, 128]]]], 'wstore': [[0, 1], [2, 3], [4, 5], [6, 7, 8]], 'wq': ['SP', 'SP', 'SP', 'SP'], 'sstore': [[0, 1, 2, 3, 4, 5, 6, 7, 8]], 'sq': [['SP', 'SP', 'SP', 'SP']], 'uwhole': True, 'bigq': {}, 'msa': 'G', 'nw': 4, 'iz': 4, 'gs': 2, 'id': 2, 'oq': ['SP', 'SP', 'SP', 'SP', 'SP', 'SP', 'SP', 'SP', 'SP']}
+ORDER = ['ms_a', 'L_g', 'warm', 'L_coef', 'ms_b', 'L_cs0', 'L_cs1', 'L_cs2', 'L_cs3', 'L_vcs3', 'L_us0', 'L_vc0', 'L_uss3', 'L_vcs0', 'F_cw', 'L_vcs2', 'W', 'L_vcs1', 'L_uc0', 'F_cs', 'L_uss0', 'L_vs0', 'gain', 'L_vss2', 'F_us0', 'L_uss2', 'F_us1', 'L_vss3', 'L_vss1', 'L_vss0', 'L_vc1', 'M1_0c0', 'M1_1c1', 'A_0c0', 'M1_0c1', 'A_1c1', 'M1_1c0', 'L_ucs1', 'F_uc0', 'L_vs1', 'A_1c0', 'A_0c1', 'L_ucs0', 'L_uss1', 'M1_0s1', 'L_ucs3', 'F_uc1', 'L_ucs2', 'L_w0_0', 'M1_0s0', 'I_1c', 'B_0c', 'L_w1_0', 'M1_1s0', 'A_0s1', 'M1_3c0', 'L_w1_1', 'M1_2c0', 'A_1s0', 'M1_1s1', 'A_3c0', 'L_w0_1', 'M1_3s1', 'A_0s0', 'M1_3s0', 'A_2c0', 'M1_2c1', 'F_us_0', 'M1_3c1', 'B_0s', 'A_3s1', 'M1_2s0', 'A_1s1', 'M2_0_0', 'A_3s0', 'F_us_1', 'M2_0_1', 'B_1s', 'A_2c1', 'C_0_0', 'M1_2s1', 'A_3c1', 'M2_1_1', 'C_0_1', 'M2_1_0', 'I_2c', 'B_1c', 'S_o0', 'A_2s0', 'M2_3_1', 'A_2s1', 'M2_3_0', 'I_3s', 'B_2c', 'M2_2_1', 'B_2s', 'C_1_0', 'M2_4_1', 'D_0_0', 'B_3s', 'M2_4_0', 'C_1_1', 'M2_2_0', 'C_3_0', 'I_3c', 'S_o1', 'M2_5_1', 'C_3_1', 'M2_5_0', 'C_2_0', 'D_1_0', 'S_o3', 'C_2_1', 'C_4_1', 'S_o2', 'D_2_0', 'C_4_0', 'B_3c', 'S_o4', 'E_1', 'D_4_0', 'M2_8_0', 'E_0', 'C_5_0', 'S_w0', 'M2_6_1', 'C_5_1', 'D_3_0', 'M2_6_0', 'C_6_1', 'S_o5', 'M2_7_0', 'C_8_0', 'D_5_0', 'C_6_0', 'S_o8', 'C_7_0', 'S_o6', 'D_8_0', 'E_2', 'S_o7', 'E_4', 'D_6_0', 'E_8', 'E_5', 'E_3', 'S_w2', 'D_7_0', 'S_w1', 'E_6', 'E_7', 'S_w3', 'S_s0_3', 'S_s0_0', 'S_s0_2', 'S_s0_1']
 
 
 def tile_fourierftgivenbases_x2_kernel(tc, w0, coef_words, coef_scales, g, uc_words, uc_scales,
@@ -83,15 +83,20 @@ def tile_fourierftgivenbases_x2_kernel(tc, w0, coef_words, coef_scales, g, uc_wo
             part = step.split("_")
             kind = part[0]
             if step == "ms_a":
-                nc.vector.memset(planes_a[:].bitcast(I32), 0)
+                (nc.gpsimd if CFG["msa"] == "G" else nc.vector).memset(planes_a[:].bitcast(I32), 0)
             elif step == "ms_b":
                 nc.vector.memset(planes_b[:].bitcast(I32), 0)
             elif step == "warm":
-                nc.gpsimd.memset(warm[:, 0:1], 0.0)
+                nc.vector.memset(warm[:, 0:1], 0.0)
                 nc.scalar.activation(out=warm[:, 1:2], in_=warm[:, 0:1], func=ACT.Copy)
             elif step == "gain":
                 nc.scalar.activation(out=gains[:, 0, :], in_=g_sb[:], func=ACT.Copy)
                 nc.scalar.activation(out=gains[:, 1, :], in_=g_sb[:], func=ACT.Copy, scale=-1.0)
+            elif step == "W":
+                bank = new_bank("warm")
+                for i in range(CFG["nw"]):
+                    nc.tensor.matmul_mx(out=bank[:], lhsT=coef_raw[:, 0:128].bitcast(FP8X4), lhsT_scale=raw_plane["cs"][:, 0:128],
+                                        rhs=coef_raw[:].bitcast(FP8X4), rhs_scale=raw_plane["cs"], start=True, stop=True)
             elif step == "L_coef":
                 nc.sync.dma_start(out=coef_raw[:].bitcast(I32), in_=words(coef_words, 0, N))
             elif step == "L_g":
@@ -155,8 +160,10 @@ def tile_fourierftgivenbases_x2_kernel(tc, w0, coef_words, coef_scales, g, uc_wo
             elif kind == "I":
                 j, b = int(part[1][0]), part[1][1]
                 mode = CFG["amode"][j]["cs".index(b)]
-                dst = z_i[(j, b)][:].rearrange("p (c i) t -> p c t i", i=CFG["iz"])
-                src = z_t[(j, b)][:].rearrange("p t (c i) -> p c t i", i=CFG["iz"])
+                w = CFG["z"][j][1]
+                c0, c1 = (0, w) if len(part) == 2 else (int(part[2]) * w // CFG["gs"], (int(part[2]) + 1) * w // CFG["gs"])
+                dst = z_i[(j, b)][:, c0:c1, :].rearrange("p (c i) t -> p c t i", i=CFG["iz"])
+                src = z_t[(j, b)][:, :, c0:c1].rearrange("p t (c i) -> p c t i", i=CFG["iz"])
                 if mode == "SV":
                     nc.vector.tensor_copy(out=dst, in_=src)
                 elif mode == "SG":
@@ -194,11 +201,12 @@ def tile_fourierftgivenbases_x2_kernel(tc, w0, coef_words, coef_scales, g, uc_wo
                         in1=w_sb[(G, wi)][:, per * k:per * k + per, c0:c0 + w], op0=ALU.mult, op1=ALU.add)
             elif kind == "D":
                 u = int(part[1])
-                dst = res_i[u][:].rearrange("p (c i) t -> p c t i", i=CFG["id"])
-                src = res[u][:].rearrange("p t (c i) -> p c t i", i=CFG["id"])
-                if CFG["units"][u][3] == "S":
+                en, c0, c1 = CFG["units"][u][3][int(part[2])]
+                dst = res_i[u][:, c0:c1, :].rearrange("p (c i) t -> p c t i", i=CFG["id"])
+                src = res[u][:, :, c0:c1].rearrange("p t (c i) -> p c t i", i=CFG["id"])
+                if en == "S":
                     nc.scalar.copy(out=dst, in_=src)
-                elif CFG["units"][u][3] == "G":
+                elif en == "G":
                     nc.gpsimd.tensor_scalar(out=dst, in0=src, scalar1=1.0, scalar2=0.0, op0=ALU.mult, op1=ALU.add)
                 else:
                     nc.vector.tensor_copy(out=dst, in_=src)

@@ -13,8 +13,8 @@ FP8X4 = mybir.dt.float8_e4m3fn_x4
 ALU = mybir.AluOpType
 ACT = mybir.ActivationFunctionType
 P = 128
-CFG = {'q': {'cs': ['SP', 'SP', 'SP', 'SP'], 'vcs': ['SP', 'SP', 'SP', 'SP'], 'vss': ['SP', 'SP', 'SP', 'SP'], 'ucs': ['SP', 'SP', 'SP', 'SP'], 'uss': ['SP', 'SP', 'G', 'G'], 'g': 'G'}, 'vload': [[0, 512], [512, 512]], 'wload': [[0, 512], [512, 512]], 'z': [[0, 256], [256, 256], [512, 256], [768, 256]], 'amode': [['V', 'V'], ['SS', 'V'], ['SS', 'V'], ['SS', 'SS']], 'units': [[0, 0, 256, [['S', 0, 256]]], [1, 0, 256, [['S', 0, 256]]], [0, 256, 256, [['S', 0, 256]]], [1, 256, 256, [['S', 0, 256]]], [0, 512, 256, [['S', 0, 256]]], [1, 512, 256, [['S', 0, 256]]], [0, 768, 256, [['S', 0, 256]]], [1, 768, 128, [['S', 0, 128]]], [1, 896, 128, [['S', 0, 128]]]], 'wstore': [[0, 1], [2, 3], [4, 5], [6, 7, 8]], 'wq': ['SP', 'SP', 'SP', 'SP'], 'sstore': [[0, 1, 2, 3, 4, 5, 6, 7, 8]], 'sq': [['SP', 'SP', 'SP', 'SP']], 'uwhole': True, 'bigq': {}, 'msa': 'G', 'nw': 4, 'iz': 4, 'gs': 2, 'id': 2, 'oq': ['SP', 'SP', 'SP', 'SP', 'SP', 'SP', 'SP', 'SP', 'SP']}
-ORDER = ['ms_a', 'L_g', 'warm', 'L_coef', 'ms_b', 'L_cs0', 'L_cs1', 'L_cs2', 'L_cs3', 'L_vcs3', 'L_us0', 'L_vc0', 'L_uss3', 'L_vcs0', 'F_cw', 'L_vcs2', 'W', 'L_vcs1', 'L_uc0', 'F_cs', 'L_uss0', 'L_vs0', 'gain', 'L_vss2', 'F_us0', 'L_uss2', 'F_us1', 'L_vss3', 'L_vss1', 'L_vss0', 'L_vc1', 'M1_0c0', 'M1_1c1', 'A_0c0', 'M1_0c1', 'A_1c1', 'M1_1c0', 'L_ucs1', 'F_uc0', 'L_vs1', 'A_1c0', 'A_0c1', 'L_ucs0', 'L_uss1', 'M1_0s1', 'L_ucs3', 'F_uc1', 'L_ucs2', 'L_w0_0', 'M1_0s0', 'I_1c', 'B_0c', 'L_w1_0', 'M1_1s0', 'A_0s1', 'M1_3c0', 'L_w1_1', 'M1_2c0', 'A_1s0', 'M1_1s1', 'A_3c0', 'L_w0_1', 'M1_3s1', 'A_0s0', 'M1_3s0', 'A_2c0', 'M1_2c1', 'F_us_0', 'M1_3c1', 'B_0s', 'A_3s1', 'M1_2s0', 'A_1s1', 'M2_0_0', 'A_3s0', 'F_us_1', 'M2_0_1', 'B_1s', 'A_2c1', 'C_0_0', 'M1_2s1', 'A_3c1', 'M2_1_1', 'C_0_1', 'M2_1_0', 'I_2c', 'B_1c', 'S_o0', 'A_2s0', 'M2_3_1', 'A_2s1', 'M2_3_0', 'I_3s', 'B_2c', 'M2_2_1', 'B_2s', 'C_1_0', 'M2_4_1', 'D_0_0', 'B_3s', 'M2_4_0', 'C_1_1', 'M2_2_0', 'C_3_0', 'I_3c', 'S_o1', 'M2_5_1', 'C_3_1', 'M2_5_0', 'C_2_0', 'D_1_0', 'S_o3', 'C_2_1', 'C_4_1', 'S_o2', 'D_2_0', 'C_4_0', 'B_3c', 'S_o4', 'E_1', 'D_4_0', 'M2_8_0', 'E_0', 'C_5_0', 'S_w0', 'M2_6_1', 'C_5_1', 'D_3_0', 'M2_6_0', 'C_6_1', 'S_o5', 'M2_7_0', 'C_8_0', 'D_5_0', 'C_6_0', 'S_o8', 'C_7_0', 'S_o6', 'D_8_0', 'E_2', 'S_o7', 'E_4', 'D_6_0', 'E_8', 'E_5', 'E_3', 'S_w2', 'D_7_0', 'S_w1', 'E_6', 'E_7', 'S_w3', 'S_s0_3', 'S_s0_0', 'S_s0_2', 'S_s0_1']
+CFG = {'q': {'cs': ['SP', 'SP', 'SP', 'SP'], 'vcs': ['SP', 'SP', 'SP', 'SP'], 'vss': ['SP', 'SP', 'SP', 'SP'], 'ucs': ['SP', 'SP', 'SP', 'SP'], 'uss': ['SP', 'SP', 'G', 'G'], 'g': 'G'}, 'vload': [[0, 512], [512, 512]], 'wload': [[0, 2, 0, 1024], [2, 4, 0, 1024]], 'z': [[0, 256], [256, 256], [512, 256], [768, 256]], 'amode': [['V', 'V'], ['SS', 'V'], ['SS', 'V'], ['SS', 'SS']], 'units': [[0, 0, 256, [['S', 0, 256]], [[0, 256]]], [1, 0, 256, [['S', 0, 256]], [[0, 256]]], [0, 256, 256, [['S', 0, 256]], [[0, 256]]], [1, 256, 256, [['S', 0, 256]], [[0, 256]]], [0, 512, 256, [['S', 0, 256]], [[0, 256]]], [1, 512, 256, [['S', 0, 256]], [[0, 256]]], [0, 768, 256, [['S', 0, 256]], [[0, 256]]], [1, 768, 256, [['S', 0, 128], ['V', 128, 256]], [[0, 128], [128, 256]]]], 'wstore': [[0, 1, 0, 512], [1, 2, 0, 512], [0, 1, 512, 1024], [1, 2, 512, 768], [1, 2, 768, 1024]], 'sstore': [[0, 2, 0, 1024]], 'uwhole': True, 'bigq': {}, 'msa': 'G', 'nw': 4, 'ostore': [[0, 0, 2, 0, 512], [0, 2, 4, 0, 512], [1, 0, 2, 0, 512], [1, 2, 4, 0, 512], [0, 0, 2, 512, 1024], [0, 2, 4, 512, 1024], [1, 0, 2, 512, 1024], [1, 2, 4, 512, 1024]], 'iz': 4, 'gs': 2, 'id': 2, 'rows': {'cs': 0, 'vcs': 4, 'vss': 8, 'ucs': 12, 'uss': 4}}
+ORDER = ['ms_a', 'L_g', 'warm', 'L_coef', 'ms_b', 'L_cs3', 'L_cs0', 'L_cs2', 'L_cs1', 'L_vcs2', 'L_vc0', 'L_us0', 'L_uss3', 'L_uss2', 'L_vcs3', 'F_cw', 'L_vcs0', 'W', 'L_vcs1', 'L_uc0', 'F_cs', 'L_vss0', 'L_vss1', 'gain', 'L_vs0', 'L_vss3', 'F_us0', 'L_vss2', 'L_ucs3', 'L_vc1', 'M1_0c1', 'F_us1', 'M1_1c0', 'A_0c1', 'M1_0c0', 'A_1c0', 'M1_1c1', 'L_ucs0', 'F_uc1', 'L_vs1', 'L_uss1', 'A_1c1', 'A_0c0', 'L_ucs1', 'L_ucs2', 'F_uc0', 'M1_1s0', 'L_uss0', 'L_w1_0', 'I_1c', 'M1_0s0', 'B_0c', 'M1_1s1', 'A_1s0', 'L_w0_1', 'M1_3c1', 'L_w0_0', 'A_0s0', 'M1_2c0', 'A_3c1', 'M1_3c0', 'L_w1_1', 'B_1c', 'M1_0s1', 'A_1s1', 'M1_3s0', 'A_3c0', 'M1_2s0', 'F_us_0', 'M1_2c1', 'A_2c0', 'B_1s', 'M1_3s1', 'M1_2s1', 'A_0s1', 'A_2c1', 'M2_2_0', 'F_us_1', 'A_3s0', 'M2_2_1', 'B_0s', 'A_2s0', 'A_3s1', 'M2_1_0', 'A_2s1', 'I_3c', 'M2_3_0', 'C_1_0', 'M2_1_1', 'C_3_0', 'M2_0_1', 'I_2c', 'C_2_1', 'S_o2', 'M2_3_1', 'B_2s', 'M2_0_0', 'C_0_1', 'I_3s', 'C_2_0', 'S_o1', 'B_2c', 'D_2_0', 'C_0_0', 'M2_4_0', 'C_3_1', 'S_o0', 'M2_5_1', 'B_3c', 'D_0_0', 'M2_5_0', 'C_1_1', 'M2_4_1', 'B_3s', 'S_o3', 'E_2_0', 'D_3_0', 'M2_6_0', 'E_0_0', 'C_4_0', 'M2_6_1', 'S_w0', 'C_6_0', 'D_1_0', 'M2_7_1', 'C_4_1', 'M2_7_0', 'S_o4', 'C_6_1', 'D_4_0', 'C_7_0', 'S_o5', 'C_5_0', 'D_6_0', 'C_7_1', 'S_o6', 'C_5_1', 'D_7_0', 'D_7_1', 'S_o7', 'E_3_0', 'D_5_0', 'E_7_1', 'E_7_0', 'E_6_0', 'E_4_0', 'E_1_0', 'S_w2', 'E_5_0', 'S_s0_2', 'S_s0_1', 'S_s0_3', 'S_w1', 'S_w4', 'S_w3', 'S_s0_0']
 
 
 def tile_fourierftgivenbases_x2_kernel(tc, w0, coef_words, coef_scales, g, uc_words, uc_scales,
@@ -34,7 +34,7 @@ def tile_fourierftgivenbases_x2_kernel(tc, w0, coef_words, coef_scales, g, uc_wo
         planes_b = sb("planes_b", [P, F + D], U8)
         raw_plane = {"cs": planes_a[:, 0:N], "vcs": planes_a[:, N:], "vss": planes_b[:, 0:F],
                      "ucs": planes_b[:, F:], "uss": planes_b[:, F:]}
-        plane_row = {"cs": 0, "vcs": 0, "vss": 0, "ucs": 0, "uss": 4}
+        plane_row = CFG["rows"]
         plane_src = {"cs": coef_scales, "vcs": vc_scales, "vss": vs_scales, "ucs": uc_scales, "uss": us_scales}
         coef_raw = sb("coef_raw", [P, N], U32)
         coef_w = sb("coef_w", [P, N], U32)
@@ -48,13 +48,13 @@ def tile_fourierftgivenbases_x2_kernel(tc, w0, coef_words, coef_scales, g, uc_wo
         g_sb = sb("g_sb", [P, 4], BF16)
         gains = sb("gains", [P, 2, 4], F32)
         warm = sb("warm", [P, 2], F32)
-        w_sb = {(G, i): sb("w_sb%d_%d" % (G, i), [P, 4, w], BF16) for G in range(2) for i, (f0, w) in enumerate(CFG["wload"])}
+        w_sb = [sb("w_sb%d" % G, [P, 4, F], BF16) for G in range(2)]
         z_t = {(j, b): sb("z_t%d%s" % (j, b), [P, 4, w], BF16) for j, (f0, w) in enumerate(CFG["z"]) for b in "cs"
                if CFG["amode"][j]["cs".index(b)] != "V"}
         z_i = {(j, b): sb("z_i%d%s" % (j, b), [P, w, 4], BF16) for j, (f0, w) in enumerate(CFG["z"]) for b in "cs"}
-        z_w = {(j, b): sb("z_w%d%s" % (j, b), [P, w], U32) for j, (f0, w) in enumerate(CFG["z"]) for b in "cs"}
-        z_s = {(j, b): sb("z_s%d%s" % (j, b), [P, w], U8) for j, (f0, w) in enumerate(CFG["z"]) for b in "cs"}
-        res = [sb("res%d" % u, [P, 4, un[2]], F32) for u, un in enumerate(CFG["units"])]
+        z_w = {b: sb("z_w" + b, [P, F], U32) for b in "cs"}
+        z_s = {b: sb("z_s" + b, [P, F], U8) for b in "cs"}
+        res = [sb("res%d" % G, [P, 4, F], F32) for G in range(2)]
         res_i = [sb("res_i%d" % u, [P, un[2], 4], BF16) for u, un in enumerate(CFG["units"])]
         out_w = sb("out_w", [P, 2, F], U32)
         out_s = sb("out_s", [P, 2, F], U8)
@@ -67,14 +67,14 @@ def tile_fourierftgivenbases_x2_kernel(tc, w0, coef_words, coef_scales, g, uc_wo
             banks[key] = bank
             return bank
 
-        def find(ranges, f):
-            return [i for i, r in enumerate(ranges) if r[0] <= f < r[0] + r[1]][0]
-
         def words(ap, c0, c1):
             return ap[0].rearrange("p n t -> p (n t)")[:, 4 * c0:4 * c1].bitcast(I32)
 
         def permute(dst, src):
             nc.vector.tensor_copy(out=dst.rearrange("p (t m) -> p m t", t=4), in_=src.rearrange("p (m t) -> p m t", t=4))
+
+        def permute_bytes(dst, src):
+            nc.vector.tensor_copy(out=dst.rearrange("p (t m) -> p t m", t=4), in_=src.rearrange("p (m t) -> p t m", t=4))
 
         def bigq(n):
             return queue[CFG["bigq"].get(n, "SP")]
@@ -117,16 +117,16 @@ def tile_fourierftgivenbases_x2_kernel(tc, w0, coef_words, coef_scales, g, uc_wo
                 bigq(part[1]).dma_start(out=v_w[b][:, f0:f0 + w].bitcast(I32), in_=words(v_src[b], f0, f0 + w))
             elif kind == "L":
                 G, i = int(part[1][1]), int(part[2])
-                f0, w = CFG["wload"][i]
-                bigq("w%d_%d" % (G, i)).dma_start(
-                    out=w_sb[(G, i)][:], in_=w0[512 * G:512 * G + 512, f0:f0 + w].rearrange("(p t) f -> p t f", t=4))
+                t0, t1, f0, f1 = CFG["wload"][i]
+                nc.sync.dma_start(out=w_sb[G][:, t0:t1, f0:f1],
+                                  in_=w0[512 * G:512 * G + 512, :].rearrange("(p t) f -> p t f", t=4)[:, t0:t1, f0:f1])
             elif step == "F_cw":
                 permute(coef_w[:].bitcast(I32), coef_raw[:].bitcast(I32))
             elif step == "F_cs":
-                permute(coef_s[:], raw_plane["cs"])
+                permute_bytes(coef_s[:], raw_plane["cs"])
             elif kind == "F" and len(part) == 3:
                 G = int(part[2])
-                permute(u_s[:, 512 * G:512 * G + 512], raw_plane["ucs"][:, 512 * G:512 * G + 512])
+                permute_bytes(u_s[:, 512 * G:512 * G + 512], raw_plane["ucs"][:, 512 * G:512 * G + 512])
             elif kind == "F":
                 b, G = part[1][1], int(part[1][2])
                 permute(u_w[b][:, 512 * G:512 * G + 512].bitcast(I32), u_raw[b][:, 512 * G:512 * G + 512].bitcast(I32))
@@ -145,7 +145,7 @@ def tile_fourierftgivenbases_x2_kernel(tc, w0, coef_words, coef_scales, g, uc_wo
                         nc.tensor.matmul_mx(
                             out=bank[:, i * n:(i + 1) * n],
                             lhsT=coef_w[:, 128 * t:128 * t + 128].bitcast(FP8X4), lhsT_scale=coef_s[:, 128 * t:128 * t + 128],
-                            rhs=v_w[b][:, c0:c0 + n].bitcast(FP8X4), rhs_scale=raw_plane["v" + b + "s"][:, c0:c0 + n],
+                            rhs=v_w[b][:, c0:c0 + n].bitcast(FP8X4), rhs_scale=raw_plane["v" + b + "s"][plane_row["v" + b + "s"]:, c0:c0 + n],
                             start=True, stop=True)
                 elif direct:
                     bi = "cs".index(b)
@@ -172,16 +172,15 @@ def tile_fourierftgivenbases_x2_kernel(tc, w0, coef_words, coef_scales, g, uc_wo
                     nc.scalar.copy(out=dst, in_=src)
             elif kind == "B":
                 j, b = int(part[1][0]), part[1][1]
-                nc.vector.quantize_mx(out=z_w[(j, b)][:].bitcast(FP8X4), scales=z_s[(j, b)][:],
+                f0, w = CFG["z"][j]
+                nc.vector.quantize_mx(out=z_w[b][:, f0:f0 + w].bitcast(FP8X4), scales=z_s[b][:, f0:f0 + w],
                                       in_=z_i[(j, b)][:].rearrange("p n t -> p (n t)"))
             elif kind in ("M2", "C"):
                 u, k = int(part[1]), int(part[2])
-                G, f0, w, dm = CFG["units"][u]
+                G, f0, w, dm, ep = CFG["units"][u]
                 per = 512 // w
                 ts = range(per * k, per * k + per)
                 if kind == "M2":
-                    j = find(CFG["z"], f0)
-                    c0 = f0 - CFG["z"][j][0]
                     bank = new_bank((2, u, k))
                     for i, t in enumerate(ts):
                         m0 = 512 * G + 128 * t
@@ -190,20 +189,19 @@ def tile_fourierftgivenbases_x2_kernel(tc, w0, coef_words, coef_scales, g, uc_wo
                                 out=bank[:, i * w:(i + 1) * w],
                                 lhsT=u_w[b][:, m0:m0 + 128].bitcast(FP8X4),
                                 lhsT_scale=u_s[plane_row["u" + b + "s"]:, m0:m0 + 128],
-                                rhs=z_w[(j, b)][:, c0:c0 + w].bitcast(FP8X4), rhs_scale=z_s[(j, b)][:, c0:c0 + w],
+                                rhs=z_w[b][:, f0:f0 + w].bitcast(FP8X4), rhs_scale=z_s[b][:, f0:f0 + w],
                                 start=(b == "c"), stop=(b == "s"))
                 else:
-                    wi = find(CFG["wload"], f0)
-                    c0 = f0 - CFG["wload"][wi][0]
                     nc.vector.scalar_tensor_tensor(
-                        out=res[u][:, per * k:per * k + per, :],
+                        out=res[G][:, per * k:per * k + per, f0:f0 + w],
                         in0=banks[(2, u, k)][:].rearrange("p (t n) -> p t n", t=per), scalar=0.5,
-                        in1=w_sb[(G, wi)][:, per * k:per * k + per, c0:c0 + w], op0=ALU.mult, op1=ALU.add)
+                        in1=w_sb[G][:, per * k:per * k + per, f0:f0 + w], op0=ALU.mult, op1=ALU.add)
             elif kind == "D":
                 u = int(part[1])
-                en, c0, c1 = CFG["units"][u][3][int(part[2])]
+                G, f0, w, dm, ep = CFG["units"][u]
+                en, c0, c1 = dm[int(part[2])]
                 dst = res_i[u][:, c0:c1, :].rearrange("p (c i) t -> p c t i", i=CFG["id"])
-                src = res[u][:, :, c0:c1].rearrange("p t (c i) -> p c t i", i=CFG["id"])
+                src = res[G][:, :, f0 + c0:f0 + c1].rearrange("p t (c i) -> p c t i", i=CFG["id"])
                 if en == "S":
                     nc.scalar.copy(out=dst, in_=src)
                 elif en == "G":
@@ -212,27 +210,20 @@ def tile_fourierftgivenbases_x2_kernel(tc, w0, coef_words, coef_scales, g, uc_wo
                     nc.vector.tensor_copy(out=dst, in_=src)
             elif kind == "E":
                 u = int(part[1])
-                G, f0, w, dm = CFG["units"][u]
-                nc.vector.quantize_mx(out=out_w[:, G, f0:f0 + w].bitcast(FP8X4), scales=out_s[:, G, f0:f0 + w],
-                                      in_=res_i[u][:].rearrange("p n t -> p (n t)"))
+                G, f0, w, dm, ep = CFG["units"][u]
+                c0, c1 = ep[int(part[2])]
+                nc.vector.quantize_mx(out=out_w[:, G, f0 + c0:f0 + c1].bitcast(FP8X4), scales=out_s[:, G, f0 + c0:f0 + c1],
+                                      in_=res_i[u][:, c0:c1, :].rearrange("p n t -> p (n t)"))
             elif part[1][0] == "o":
-                u = int(part[1][1:])
-                G, f0, w, dm = CFG["units"][u]
-                queue[CFG["oq"][u]].dma_start(
-                    out=out_0[512 * G:512 * G + 512, f0:f0 + w].rearrange("(p t) f -> p t f", t=4), in_=res[u][:])
+                G, t0, t1, f0, f1 = CFG["ostore"][int(part[1][1:])]
+                nc.sync.dma_start(out=out_0[512 * G:512 * G + 512, :].rearrange("(p t) f -> p t f", t=4)[:, t0:t1, f0:f1],
+                                  in_=res[G][:, t0:t1, f0:f1])
+            elif part[1][0] == "w":
+                G0, G1, f0, f1 = CFG["wstore"][int(part[1][1:])]
+                nc.sync.dma_start(out=out_1[G0:G1].rearrange("g p f t -> p g (f t)")[:, :, 4 * f0:4 * f1].bitcast(I32),
+                                  in_=out_w[:, G0:G1, f0:f1].bitcast(I32))
             else:
-                s = int(part[1][1:])
-                us = CFG["wstore" if part[1][0] == "w" else "sstore"][s]
-                Gs = sorted(set(CFG["units"][u][0] for u in us))
-                f0 = min(CFG["units"][u][1] for u in us)
-                f1 = max(CFG["units"][u][1] + CFG["units"][u][2] for u in us)
-                G0, G1 = Gs[0], Gs[-1] + 1
-                if part[1][0] == "w":
-                    queue[CFG["wq"][s]].dma_start(
-                        out=out_1[G0:G1].rearrange("g p f t -> p g (f t)")[:, :, 4 * f0:4 * f1].bitcast(I32),
-                        in_=out_w[:, G0:G1, f0:f1].bitcast(I32))
-                else:
-                    Q = int(part[2])
-                    queue[CFG["sq"][s][Q]].dma_start(
-                        out=out_2[G0:G1, 4 * Q:4 * Q + 4, f0:f1].rearrange("g r f -> r g f").bitcast(I32),
-                        in_=out_s[32 * Q:32 * Q + 4, G0:G1, f0:f1].bitcast(I32))
+                G0, G1, f0, f1 = CFG["sstore"][int(part[1][1:])]
+                Q = int(part[2])
+                nc.sync.dma_start(out=out_2[G0:G1, 4 * Q:4 * Q + 4, f0:f1].rearrange("g r f -> r g f").bitcast(I32),
+                                  in_=out_s[32 * Q:32 * Q + 4, G0:G1, f0:f1].bitcast(I32))

@@ -4,6 +4,8 @@ import concourse.mybir as mybir
 
 D, F, N = 1024, 1024, 512
 FLOPS = 2 * (2 * N * N * F) + 2 * (2 * D * N * F)
+ALPHA = 0.5
+
 F32 = mybir.dt.float32
 BF16 = mybir.dt.bfloat16
 I32 = mybir.dt.int32
@@ -12,218 +14,280 @@ U8 = mybir.dt.uint8
 FP8X4 = mybir.dt.float8_e4m3fn_x4
 ALU = mybir.AluOpType
 ACT = mybir.ActivationFunctionType
+
 P = 128
-CFG = {'q': {'cs': ['SP', 'SP', 'SP', 'SP'], 'vcs': ['SP', 'SP', 'SP', 'SP'], 'vss': ['SP', 'SP', 'SP', 'SP'], 'ucs': ['SP', 'SP', 'SP', 'SP'], 'uss': ['SP', 'SP', 'G', 'G'], 'g': 'G'}, 'vload': [[0, 512], [512, 512]], 'wload': [[0, 2, 0, 1024], [2, 4, 0, 1024]], 'z': [[0, 256], [256, 256], [512, 256], [768, 256]], 'amode': [['V', 'V'], ['SS', 'V'], ['SS', 'V'], ['SS', 'SS']], 'units': [[0, 0, 256, [['S', 0, 256]], [[0, 256]]], [1, 0, 256, [['S', 0, 256]], [[0, 256]]], [0, 256, 256, [['S', 0, 256]], [[0, 256]]], [1, 256, 256, [['S', 0, 256]], [[0, 256]]], [0, 512, 256, [['S', 0, 256]], [[0, 256]]], [1, 512, 256, [['S', 0, 256]], [[0, 256]]], [0, 768, 256, [['S', 0, 256]], [[0, 256]]], [1, 768, 256, [['S', 0, 128], ['V', 128, 256]], [[0, 128], [128, 256]]]], 'wstore': [[0, 1, 0, 512], [1, 2, 0, 512], [0, 1, 512, 1024], [1, 2, 512, 768], [1, 2, 768, 1024]], 'sstore': [[0, 2, 0, 1024]], 'uwhole': True, 'bigq': {}, 'msa': 'G', 'nw': 4, 'ostore': [[0, 0, 2, 0, 512], [0, 2, 4, 0, 512], [1, 0, 2, 0, 512], [1, 2, 4, 0, 512], [0, 0, 2, 512, 1024], [0, 2, 4, 512, 1024], [1, 0, 2, 512, 1024], [1, 2, 4, 512, 1024]], 'iz': 4, 'gs': 2, 'id': 2, 'rows': {'cs': 0, 'vcs': 4, 'vss': 8, 'ucs': 12, 'uss': 4}}
-ORDER = ['ms_a', 'L_g', 'warm', 'L_coef', 'ms_b', 'L_cs3', 'L_cs0', 'L_cs2', 'L_cs1', 'L_vcs2', 'L_vc0', 'L_us0', 'L_uss3', 'L_uss2', 'L_vcs3', 'F_cw', 'L_vcs0', 'W', 'L_vcs1', 'L_uc0', 'F_cs', 'L_vss0', 'L_vss1', 'gain', 'L_vs0', 'L_vss3', 'F_us0', 'L_vss2', 'L_ucs3', 'L_vc1', 'M1_0c1', 'F_us1', 'M1_1c0', 'A_0c1', 'M1_0c0', 'A_1c0', 'M1_1c1', 'L_ucs0', 'F_uc1', 'L_vs1', 'L_uss1', 'A_1c1', 'A_0c0', 'L_ucs1', 'L_ucs2', 'F_uc0', 'M1_1s0', 'L_uss0', 'L_w1_0', 'I_1c', 'M1_0s0', 'B_0c', 'M1_1s1', 'A_1s0', 'L_w0_1', 'M1_3c1', 'L_w0_0', 'A_0s0', 'M1_2c0', 'A_3c1', 'M1_3c0', 'L_w1_1', 'B_1c', 'M1_0s1', 'A_1s1', 'M1_3s0', 'A_3c0', 'M1_2s0', 'F_us_0', 'M1_2c1', 'A_2c0', 'B_1s', 'M1_3s1', 'M1_2s1', 'A_0s1', 'A_2c1', 'M2_2_0', 'F_us_1', 'A_3s0', 'M2_2_1', 'B_0s', 'A_2s0', 'A_3s1', 'M2_1_0', 'A_2s1', 'I_3c', 'M2_3_0', 'C_1_0', 'M2_1_1', 'C_3_0', 'M2_0_1', 'I_2c', 'C_2_1', 'S_o2', 'M2_3_1', 'B_2s', 'M2_0_0', 'C_0_1', 'I_3s', 'C_2_0', 'S_o1', 'B_2c', 'D_2_0', 'C_0_0', 'M2_4_0', 'C_3_1', 'S_o0', 'M2_5_1', 'B_3c', 'D_0_0', 'M2_5_0', 'C_1_1', 'M2_4_1', 'B_3s', 'S_o3', 'E_2_0', 'D_3_0', 'M2_6_0', 'E_0_0', 'C_4_0', 'M2_6_1', 'S_w0', 'C_6_0', 'D_1_0', 'M2_7_1', 'C_4_1', 'M2_7_0', 'S_o4', 'C_6_1', 'D_4_0', 'C_7_0', 'S_o5', 'C_5_0', 'D_6_0', 'C_7_1', 'S_o6', 'C_5_1', 'D_7_0', 'D_7_1', 'S_o7', 'E_3_0', 'D_5_0', 'E_7_1', 'E_7_0', 'E_6_0', 'E_4_0', 'E_1_0', 'S_w2', 'E_5_0', 'S_s0_2', 'S_s0_1', 'S_s0_3', 'S_w1', 'S_w4', 'S_w3', 'S_s0_0']
+PACK = 4
+PASS = P * PACK
+QUADRANT = 32
+BANKS = 8
+BANK = 512
+CHUNK = 256
+HALF = 512
+COS, SIN = 0, 1
+SIGN = (1.0, -1.0)
+SCALE_ROW = {"coef": 0, "vc": 4, "vs": 8, "uc": 12, "us": 4}
 
 
 def tile_fourierftgivenbases_x2_kernel(tc, w0, coef_words, coef_scales, g, uc_words, uc_scales,
                                                   us_words, us_scales, vc_words, vc_scales, vs_words, vs_scales,
                                                   out_0, out_1, out_2):
     nc = tc.nc
-    queue = {"SP": nc.sync, "S": nc.scalar, "G": nc.gpsimd}
+    chunks, groups, halves = F // CHUNK, D // PASS, F // HALF
+
     with ExitStack() as ctx:
         keep = ctx.enter_context(tc.tile_pool(name="keep", bufs=1))
         psum = ctx.enter_context(tc.psum_pool(name="psum", bufs=1))
         ctx.enter_context(tc.manual_schedule())
 
-        def sb(name, shape, dtype):
+        def sbuf(name, shape, dtype):
             return keep.tile(shape, dtype, name=name, align_bytes=256)
 
-        planes_a = sb("planes_a", [P, N + F], U8)
-        planes_b = sb("planes_b", [P, F + D], U8)
-        raw_plane = {"cs": planes_a[:, 0:N], "vcs": planes_a[:, N:], "vss": planes_b[:, 0:F],
-                     "ucs": planes_b[:, F:], "uss": planes_b[:, F:]}
-        plane_row = CFG["rows"]
-        plane_src = {"cs": coef_scales, "vcs": vc_scales, "vss": vs_scales, "ucs": uc_scales, "uss": us_scales}
-        coef_raw = sb("coef_raw", [P, N], U32)
-        coef_w = sb("coef_w", [P, N], U32)
-        coef_s = sb("coef_s", [P, N], U8)
-        u_raw = {b: sb("u_raw" + b, [P, D], U32) for b in "cs"}
-        u_w = {b: sb("u_w" + b, [P, D], U32) for b in "cs"}
-        u_s = sb("u_s", [P, D], U8)
-        v_w = {b: sb("v_w" + b, [P, F], U32) for b in "cs"}
-        u_src = {"c": uc_words, "s": us_words}
-        v_src = {"c": vc_words, "s": vs_words}
-        g_sb = sb("g_sb", [P, 4], BF16)
-        gains = sb("gains", [P, 2, 4], F32)
-        warm = sb("warm", [P, 2], F32)
-        w_sb = [sb("w_sb%d" % G, [P, 4, F], BF16) for G in range(2)]
-        z_t = {(j, b): sb("z_t%d%s" % (j, b), [P, 4, w], BF16) for j, (f0, w) in enumerate(CFG["z"]) for b in "cs"
-               if CFG["amode"][j]["cs".index(b)] != "V"}
-        z_i = {(j, b): sb("z_i%d%s" % (j, b), [P, w, 4], BF16) for j, (f0, w) in enumerate(CFG["z"]) for b in "cs"}
-        z_w = {b: sb("z_w" + b, [P, F], U32) for b in "cs"}
-        z_s = {b: sb("z_s" + b, [P, F], U8) for b in "cs"}
-        res = [sb("res%d" % G, [P, 4, F], F32) for G in range(2)]
-        res_i = [sb("res_i%d" % u, [P, un[2], 4], BF16) for u, un in enumerate(CFG["units"])]
-        out_w = sb("out_w", [P, 2, F], U32)
-        out_s = sb("out_s", [P, 2, F], U8)
+        coef_raw_s = sbuf("coef_raw_s", [P, N], U8)
+        vc_s = sbuf("vc_s", [P, F], U8)
+        vs_u_s = sbuf("vs_u_s", [P, F + D], U8)
+        raw_s = {"coef": coef_raw_s[:], "vc": vc_s[:], "vs": vs_u_s[:, :F], "uc": vs_u_s[:, F:], "us": vs_u_s[:, F:]}
+        hbm_s = {"coef": coef_scales, "vc": vc_scales, "vs": vs_scales, "uc": uc_scales, "us": us_scales}
+        coef_raw_w = sbuf("coef_raw_w", [P, N], U32)
+        coef_w = sbuf("coef_w", [P, N], U32)
+        coef_s = sbuf("coef_s", [P, N], U8)
+        u_raw_w = [sbuf("u_raw_w%d" % b, [P, D], U32) for b in (COS, SIN)]
+        u_w = [sbuf("u_w%d" % b, [P, D], U32) for b in (COS, SIN)]
+        u_s = sbuf("u_s", [P, D], U8)
+        v_w = [sbuf("v_w%d" % b, [P, F], U32) for b in (COS, SIN)]
+        v_s = [raw_s[name][SCALE_ROW[name]:, :] for name in ("vc", "vs")]
+        u_s_rows = [u_s[SCALE_ROW[name]:, :] for name in ("uc", "us")]
+        gain_bf = sbuf("gain_bf", [P, PACK], BF16)
+        gain = sbuf("gain", [P, 2, PACK], F32)
+        base = [sbuf("base%d" % G, [P, PACK, F], BF16) for G in range(groups)]
+        z_rows = {key: sbuf("z_rows%d_%d" % key, [P, PACK, CHUNK], BF16) for key in ((1, COS), (2, COS), (3, COS), (3, SIN))}
+        z_side = [sbuf("z_side%d" % j, [P, 2, CHUNK, PACK], BF16) for j in range(chunks)]
+        z_w = sbuf("z_w", [P, chunks, 2, CHUNK], U32)
+        z_s = sbuf("z_s", [P, chunks, 2, CHUNK], U8)
+        res = {(G, h): sbuf("res%d_%d" % (G, h), [P, PACK, HALF], F32) for h in range(halves) for G in range(groups)}
+        res_side = {(G, h): sbuf("res_side%d_%d" % (G, h), [P, HALF, PACK], BF16)
+                    for h in range(halves) for G in range(groups)}
+        out_w = sbuf("out_w", [P, groups, F], U32)
+        out_s = sbuf("out_s", [P, groups, F], U8)
+
         banks = {}
-        count = []
 
-        def new_bank(key):
-            bank = psum.tile([P, 512], F32, name="bank%d" % (len(count) % 8))
-            count.append(key)
-            banks[key] = bank
-            return bank
+        def next_bank(key):
+            banks[key] = psum.tile([P, BANK], F32, name="bank%d" % (len(banks) % BANKS))
+            return banks[key]
 
-        def words(ap, c0, c1):
-            return ap[0].rearrange("p n t -> p (n t)")[:, 4 * c0:4 * c1].bitcast(I32)
+        def places(t, group=0):
+            return slice(PASS * group + P * t, PASS * group + P * (t + 1))
 
-        def permute(dst, src):
-            nc.vector.tensor_copy(out=dst.rearrange("p (t m) -> p m t", t=4), in_=src.rearrange("p (m t) -> p m t", t=4))
+        def row_view(hbm, G):
+            return hbm[PASS * G:PASS * (G + 1), :].rearrange("(p t) f -> p t f", t=PACK)
 
-        def permute_bytes(dst, src):
-            nc.vector.tensor_copy(out=dst.rearrange("p (t m) -> p t m", t=4), in_=src.rearrange("p (m t) -> p t m", t=4))
+        def load_words(dst, hbm, c0, c1):
+            nc.sync.dma_start(out=dst[:, c0:c1].bitcast(I32),
+                              in_=hbm[0].rearrange("p n t -> p (n t)")[:, PACK * c0:PACK * c1].bitcast(I32))
 
-        def bigq(n):
-            return queue[CFG["bigq"].get(n, "SP")]
+        def load_scales(name, rows, queue=nc.sync):
+            for r in rows:
+                queue.dma_start(out=raw_s[name][SCALE_ROW[name] + r:P:QUADRANT, :].bitcast(I32),
+                                in_=hbm_s[name][0, r:16:4, :].bitcast(I32))
 
-        for step in ORDER:
-            part = step.split("_")
-            kind = part[0]
-            if step == "ms_a":
-                (nc.gpsimd if CFG["msa"] == "G" else nc.vector).memset(planes_a[:].bitcast(I32), 0)
-            elif step == "ms_b":
-                nc.vector.memset(planes_b[:].bitcast(I32), 0)
-            elif step == "warm":
-                nc.vector.memset(warm[:, 0:1], 0.0)
-                nc.scalar.activation(out=warm[:, 1:2], in_=warm[:, 0:1], func=ACT.Copy)
-            elif step == "gain":
-                nc.scalar.activation(out=gains[:, 0, :], in_=g_sb[:], func=ACT.Copy)
-                nc.scalar.activation(out=gains[:, 1, :], in_=g_sb[:], func=ACT.Copy, scale=-1.0)
-            elif step == "W":
-                bank = new_bank("warm")
-                for i in range(CFG["nw"]):
-                    nc.tensor.matmul_mx(out=bank[:], lhsT=coef_raw[:, 0:128].bitcast(FP8X4), lhsT_scale=raw_plane["cs"][:, 0:128],
-                                        rhs=coef_raw[:].bitcast(FP8X4), rhs_scale=raw_plane["cs"], start=True, stop=True)
-            elif step == "L_coef":
-                nc.sync.dma_start(out=coef_raw[:].bitcast(I32), in_=words(coef_words, 0, N))
-            elif step == "L_g":
-                queue[CFG["q"]["g"]].dma_start(out=g_sb[:], in_=g.rearrange("(p t) -> p t", t=4))
-            elif kind == "L" and part[1][:-1] in raw_plane:
-                name, Q = part[1][:-1], int(part[1][-1])
-                q = CFG["q"][name]
-                r = 32 * Q + plane_row[name]
-                queue[q[Q]].dma_start(
-                    out=raw_plane[name][r:r + 4, :].bitcast(I32), in_=plane_src[name][0, 4 * Q:4 * Q + 4, :].bitcast(I32))
-            elif kind == "L" and part[1][0] == "u":
-                b, G = part[1][1], int(part[1][2])
-                c0, c1 = (0, D) if CFG["uwhole"] else (512 * G, 512 * G + 512)
-                bigq(part[1]).dma_start(out=u_raw[b][:, c0:c1].bitcast(I32), in_=words(u_src[b], c0, c1))
-            elif kind == "L" and part[1][0] == "v":
-                b, i = part[1][1], int(part[1][2])
-                f0, w = CFG["vload"][i]
-                bigq(part[1]).dma_start(out=v_w[b][:, f0:f0 + w].bitcast(I32), in_=words(v_src[b], f0, f0 + w))
-            elif kind == "L":
-                G, i = int(part[1][1]), int(part[2])
-                t0, t1, f0, f1 = CFG["wload"][i]
-                nc.sync.dma_start(out=w_sb[G][:, t0:t1, f0:f1],
-                                  in_=w0[512 * G:512 * G + 512, :].rearrange("(p t) f -> p t f", t=4)[:, t0:t1, f0:f1])
-            elif step == "F_cw":
-                permute(coef_w[:].bitcast(I32), coef_raw[:].bitcast(I32))
-            elif step == "F_cs":
-                permute_bytes(coef_s[:], raw_plane["cs"])
-            elif kind == "F" and len(part) == 3:
-                G = int(part[2])
-                permute_bytes(u_s[:, 512 * G:512 * G + 512], raw_plane["ucs"][:, 512 * G:512 * G + 512])
-            elif kind == "F":
-                b, G = part[1][1], int(part[1][2])
-                permute(u_w[b][:, 512 * G:512 * G + 512].bitcast(I32), u_raw[b][:, 512 * G:512 * G + 512].bitcast(I32))
-            elif kind in ("M1", "A"):
-                j, b, k = int(part[1][0]), part[1][1], int(part[1][2])
-                f0, w = CFG["z"][j]
-                direct = CFG["amode"][j]["cs".index(b)] == "V"
-                if direct:
-                    n, per, ts, c0 = 128, 4, range(4), f0 + 128 * k
-                else:
-                    per = 512 // w
-                    n, ts, c0 = w, range(per * k, per * k + per), f0
-                if kind == "M1":
-                    bank = new_bank((1, j, b, k))
-                    for i, t in enumerate(ts):
-                        nc.tensor.matmul_mx(
-                            out=bank[:, i * n:(i + 1) * n],
-                            lhsT=coef_w[:, 128 * t:128 * t + 128].bitcast(FP8X4), lhsT_scale=coef_s[:, 128 * t:128 * t + 128],
-                            rhs=v_w[b][:, c0:c0 + n].bitcast(FP8X4), rhs_scale=raw_plane["v" + b + "s"][plane_row["v" + b + "s"]:, c0:c0 + n],
-                            start=True, stop=True)
-                elif direct:
-                    bi = "cs".index(b)
-                    nc.vector.tensor_tensor(
-                        out=z_i[(j, b)][:, 128 * k:128 * k + 128, :],
-                        in0=banks[(1, j, b, k)][:].rearrange("p (t n) -> p n t", t=4),
-                        in1=gains[:, bi:bi + 1, :].broadcast_to([P, 128, 4]), op=ALU.mult)
-                else:
-                    for i, t in enumerate(ts):
-                        nc.scalar.activation(out=z_t[(j, b)][:, t, :], in_=banks[(1, j, b, k)][:, i * n:(i + 1) * n],
-                                             func=ACT.Copy, scale=gains[:, "cs".index(b), t:t + 1])
-            elif kind == "I":
-                j, b = int(part[1][0]), part[1][1]
-                mode = CFG["amode"][j]["cs".index(b)]
-                w = CFG["z"][j][1]
-                c0, c1 = (0, w) if len(part) == 2 else (int(part[2]) * w // CFG["gs"], (int(part[2]) + 1) * w // CFG["gs"])
-                dst = z_i[(j, b)][:, c0:c1, :].rearrange("p (c i) t -> p c t i", i=CFG["iz"])
-                src = z_t[(j, b)][:, :, c0:c1].rearrange("p t (c i) -> p c t i", i=CFG["iz"])
-                if mode == "SV":
-                    nc.vector.tensor_copy(out=dst, in_=src)
-                elif mode == "SG":
-                    nc.gpsimd.tensor_scalar(out=dst, in0=src, scalar1=1.0, scalar2=0.0, op0=ALU.mult, op1=ALU.add)
-                else:
-                    nc.scalar.copy(out=dst, in_=src)
-            elif kind == "B":
-                j, b = int(part[1][0]), part[1][1]
-                f0, w = CFG["z"][j]
-                nc.vector.quantize_mx(out=z_w[b][:, f0:f0 + w].bitcast(FP8X4), scales=z_s[b][:, f0:f0 + w],
-                                      in_=z_i[(j, b)][:].rearrange("p n t -> p (n t)"))
-            elif kind in ("M2", "C"):
-                u, k = int(part[1]), int(part[2])
-                G, f0, w, dm, ep = CFG["units"][u]
-                per = 512 // w
-                ts = range(per * k, per * k + per)
-                if kind == "M2":
-                    bank = new_bank((2, u, k))
-                    for i, t in enumerate(ts):
-                        m0 = 512 * G + 128 * t
-                        for b in "cs":
-                            nc.tensor.matmul_mx(
-                                out=bank[:, i * w:(i + 1) * w],
-                                lhsT=u_w[b][:, m0:m0 + 128].bitcast(FP8X4),
-                                lhsT_scale=u_s[plane_row["u" + b + "s"]:, m0:m0 + 128],
-                                rhs=z_w[b][:, f0:f0 + w].bitcast(FP8X4), rhs_scale=z_s[b][:, f0:f0 + w],
-                                start=(b == "c"), stop=(b == "s"))
-                else:
-                    nc.vector.scalar_tensor_tensor(
-                        out=res[G][:, per * k:per * k + per, f0:f0 + w],
-                        in0=banks[(2, u, k)][:].rearrange("p (t n) -> p t n", t=per), scalar=0.5,
-                        in1=w_sb[G][:, per * k:per * k + per, f0:f0 + w], op0=ALU.mult, op1=ALU.add)
-            elif kind == "D":
-                u = int(part[1])
-                G, f0, w, dm, ep = CFG["units"][u]
-                en, c0, c1 = dm[int(part[2])]
-                dst = res_i[u][:, c0:c1, :].rearrange("p (c i) t -> p c t i", i=CFG["id"])
-                src = res[G][:, :, f0 + c0:f0 + c1].rearrange("p t (c i) -> p c t i", i=CFG["id"])
-                if en == "S":
-                    nc.scalar.copy(out=dst, in_=src)
-                elif en == "G":
-                    nc.gpsimd.tensor_scalar(out=dst, in0=src, scalar1=1.0, scalar2=0.0, op0=ALU.mult, op1=ALU.add)
-                else:
-                    nc.vector.tensor_copy(out=dst, in_=src)
-            elif kind == "E":
-                u = int(part[1])
-                G, f0, w, dm, ep = CFG["units"][u]
-                c0, c1 = ep[int(part[2])]
-                nc.vector.quantize_mx(out=out_w[:, G, f0 + c0:f0 + c1].bitcast(FP8X4), scales=out_s[:, G, f0 + c0:f0 + c1],
-                                      in_=res_i[u][:, c0:c1, :].rearrange("p n t -> p (n t)"))
-            elif part[1][0] == "o":
-                G, t0, t1, f0, f1 = CFG["ostore"][int(part[1][1:])]
-                nc.sync.dma_start(out=out_0[512 * G:512 * G + 512, :].rearrange("(p t) f -> p t f", t=4)[:, t0:t1, f0:f1],
-                                  in_=res[G][:, t0:t1, f0:f1])
-            elif part[1][0] == "w":
-                G0, G1, f0, f1 = CFG["wstore"][int(part[1][1:])]
-                nc.sync.dma_start(out=out_1[G0:G1].rearrange("g p f t -> p g (f t)")[:, :, 4 * f0:4 * f1].bitcast(I32),
-                                  in_=out_w[:, G0:G1, f0:f1].bitcast(I32))
+        def load_base(G, k):
+            nc.sync.dma_start(out=base[G][:, 2 * k:2 * k + 2, :], in_=row_view(w0, G)[:, 2 * k:2 * k + 2, :])
+
+        def reorder_words(dst, src):
+            nc.vector.tensor_copy(out=dst[:].bitcast(I32).rearrange("p (g t m) -> p g m t", t=PACK, m=P),
+                                  in_=src[:].bitcast(I32).rearrange("p (g m t) -> p g m t", t=PACK, m=P))
+
+        def reorder_scales(dst, src):
+            nc.vector.tensor_copy(out=dst[:].rearrange("p (g t m) -> p g t m", t=PACK, m=P),
+                                  in_=src.rearrange("p (g m t) -> p g t m", t=PACK, m=P))
+
+        def z_matmul(out, t, b, c0, c1):
+            nc.tensor.matmul_mx(out=out, lhsT=coef_w[:, places(t)].bitcast(FP8X4), lhsT_scale=coef_s[:, places(t)],
+                                rhs=v_w[b][:, c0:c1].bitcast(FP8X4), rhs_scale=v_s[b][:, c0:c1], start=True, stop=True)
+
+        def z_bank(j, b, k):
+            bank = next_bank(("z", j, b, k))
+            if (j, b) in z_rows:
+                for i in range(2):
+                    z_matmul(bank[:, i * CHUNK:(i + 1) * CHUNK], 2 * k + i, b, j * CHUNK, (j + 1) * CHUNK)
             else:
-                G0, G1, f0, f1 = CFG["sstore"][int(part[1][1:])]
-                Q = int(part[2])
-                nc.sync.dma_start(out=out_2[G0:G1, 4 * Q:4 * Q + 4, f0:f1].rearrange("g r f -> r g f").bitcast(I32),
-                                  in_=out_s[32 * Q:32 * Q + 4, G0:G1, f0:f1].bitcast(I32))
+                for t in range(PACK):
+                    z_matmul(bank[:, places(t)], t, b, j * CHUNK + k * P, j * CHUNK + (k + 1) * P)
+
+        def z_out(j, b, k):
+            bank = banks[("z", j, b, k)]
+            if (j, b) in z_rows:
+                for i in range(2):
+                    t = 2 * k + i
+                    nc.scalar.activation(out=z_rows[(j, b)][:, t, :], in_=bank[:, i * CHUNK:(i + 1) * CHUNK],
+                                         func=ACT.Copy, scale=gain[:, b, t:t + 1])
+            else:
+                nc.vector.scalar_tensor_tensor(
+                    out=z_side[j][:, b, k * P:(k + 1) * P, :], in0=bank[:].rearrange("p (t n) -> p n t", t=PACK),
+                    scalar=SIGN[b], in1=gain_bf[:].unsqueeze(1).broadcast_to([P, P, PACK]), op0=ALU.mult, op1=ALU.mult)
+
+        def z_interleave(j, b):
+            nc.scalar.copy(out=z_side[j][:, b].rearrange("p (c i) t -> p c t i", i=4),
+                           in_=z_rows[(j, b)][:].rearrange("p t (c i) -> p c t i", i=4))
+
+        def z_quantize(j, first, count=1):
+            bases = slice(first, first + count)
+            nc.vector.quantize_mx(out=z_w[:, j, bases, :].rearrange("p b n -> p (b n)").bitcast(FP8X4),
+                                  scales=z_s[:, j, bases, :].rearrange("p b n -> p (b n)"),
+                                  in_=z_side[j][:, bases].rearrange("p b n t -> p (b n t)"))
+
+        def out_bank(G, j, k):
+            bank = next_bank(("out", G, j, k))
+            for i in range(2):
+                cols = places(2 * k + i, G)
+                for b in (COS, SIN):
+                    nc.tensor.matmul_mx(out=bank[:, i * CHUNK:(i + 1) * CHUNK],
+                                        lhsT=u_w[b][:, cols].bitcast(FP8X4), lhsT_scale=u_s_rows[b][:, cols],
+                                        rhs=z_w[:, j, b, :].bitcast(FP8X4), rhs_scale=z_s[:, j, b, :],
+                                        start=(b == COS), stop=(b == SIN))
+
+        def add_base(G, j, k):
+            h, c0 = divmod(j * CHUNK, HALF)
+            nc.vector.scalar_tensor_tensor(
+                out=res[(G, h)][:, 2 * k:2 * k + 2, c0:c0 + CHUNK],
+                in0=banks[("out", G, j, k)][:].rearrange("p (t n) -> p t n", t=2), scalar=ALPHA,
+                in1=base[G][:, 2 * k:2 * k + 2, j * CHUNK:(j + 1) * CHUNK], op0=ALU.mult, op1=ALU.add)
+
+        def store_rows(G, h, k):
+            nc.sync.dma_start(out=row_view(out_0, G)[:, 2 * k:2 * k + 2, h * HALF:(h + 1) * HALF],
+                              in_=res[(G, h)][:, 2 * k:2 * k + 2, :])
+
+        def round_result(G, h, c0, c1, copy=nc.scalar.copy):
+            copy(out=res_side[(G, h)][:, c0:c1, :].rearrange("p (c i) t -> p c t i", i=2),
+                 in_=res[(G, h)][:, :, c0:c1].rearrange("p t (c i) -> p c t i", i=2))
+
+        def quantize_result(G, h, c0, c1):
+            cols = slice(h * HALF + c0, h * HALF + c1)
+            nc.vector.quantize_mx(out=out_w[:, G, cols].bitcast(FP8X4), scales=out_s[:, G, cols],
+                                  in_=res_side[(G, h)][:, c0:c1, :].rearrange("p n t -> p (n t)"))
+
+        def store_words(G, h):
+            nc.sync.dma_start(
+                out=out_1[G].rearrange("p f t -> p (f t)")[:, PACK * HALF * h:PACK * HALF * (h + 1)].bitcast(I32),
+                in_=out_w[:, G, h * HALF:(h + 1) * HALF].bitcast(I32))
+
+        nc.gpsimd.memset(vc_s[:].bitcast(I32), 0)
+        nc.vector.memset(coef_raw_s[:].bitcast(I32), 0)
+        nc.vector.memset(vs_u_s[:].bitcast(I32), 0)
+
+        nc.gpsimd.dma_start(out=gain_bf[:], in_=g.rearrange("(p t) -> p t", t=PACK))
+        load_scales("us", (2, 3), nc.gpsimd)
+        load_words(coef_raw_w, coef_words, 0, N)
+        load_scales("coef", range(4))
+        load_scales("vc", (0,))
+        load_words(v_w[COS], vc_words, 0, HALF)
+        load_words(u_raw_w[SIN], us_words, 0, D)
+        load_scales("vc", (1, 2, 3))
+        load_words(v_w[SIN], vs_words, 0, HALF)
+        load_scales("vs", (0, 1))
+        load_words(u_raw_w[COS], uc_words, 0, D)
+        load_scales("vs", (2, 3))
+        load_scales("uc", (0,))
+        load_words(v_w[COS], vc_words, HALF, F)
+        load_scales("uc", (1, 2))
+        load_base(0, 0)
+        load_scales("uc", (3,))
+        load_scales("us", (0, 1))
+        load_words(v_w[SIN], vs_words, HALF, F)
+        load_base(0, 1)
+        load_base(1, 0)
+        load_base(1, 1)
+
+        for b in (COS, SIN):
+            nc.scalar.activation(out=gain[:, b, :], in_=gain_bf[:], func=ACT.Copy, scale=SIGN[b])
+        reorder_words(coef_w, coef_raw_w)
+        reorder_scales(coef_s, raw_s["coef"])
+        reorder_words(u_w[SIN], u_raw_w[SIN])
+
+        for j, b in ((0, COS), (1, COS), (0, SIN), (2, COS)):
+            for k in range(2):
+                z_bank(j, b, k)
+        for j in (0, 1):
+            for k in range(2):
+                z_out(j, COS, k)
+        reorder_words(u_w[COS], u_raw_w[COS])
+        z_quantize(0, COS)
+        for j, b in ((1, SIN), (3, COS)):
+            for k in range(2):
+                z_bank(j, b, k)
+        for j, b in ((0, SIN), (2, COS)):
+            for k in range(2):
+                z_out(j, b, k)
+        z_interleave(1, COS)
+        for j, k in ((2, 0), (3, 0), (3, 1), (2, 1)):
+            z_bank(j, SIN, k)
+        reorder_scales(u_s, raw_s["uc"])
+        z_quantize(0, SIN)
+        for k in range(2):
+            z_out(1, SIN, k)
+            out_bank(0, 0, k)
+        for b in (COS, SIN):
+            for k in range(2):
+                z_out(3, b, k)
+        z_out(2, SIN, 0)
+        z_quantize(1, COS)
+        z_quantize(1, SIN)
+        for j, b in ((2, COS), (3, COS), (3, SIN)):
+            z_interleave(j, b)
+
+        for k in range(2):
+            out_bank(0, 1, k)
+        add_base(0, 0, 0)
+        z_out(2, SIN, 1)
+        for k in range(2):
+            out_bank(1, 0, k)
+            out_bank(1, 1, k)
+        add_base(0, 1, 0)
+        store_rows(0, 0, 0)
+        add_base(0, 0, 1)
+        z_quantize(2, COS, 2)
+        add_base(0, 1, 1)
+        store_rows(0, 0, 1)
+        for c0 in (0, CHUNK):
+            round_result(0, 0, c0, c0 + CHUNK)
+        out_bank(0, 2, 0)
+        add_base(1, 0, 0)
+        add_base(1, 1, 0)
+        store_rows(1, 0, 0)
+        z_quantize(3, COS, 2)
+        out_bank(0, 3, 0)
+        out_bank(0, 2, 1)
+        out_bank(0, 3, 1)
+        add_base(1, 0, 1)
+        add_base(1, 1, 1)
+        store_rows(1, 0, 1)
+        for c0 in (0, CHUNK):
+            round_result(1, 0, c0, c0 + CHUNK)
+        for k in range(2):
+            out_bank(1, 2, k)
+            out_bank(1, 3, k)
+
+        for G in range(groups):
+            for k in range(2):
+                add_base(G, 2, k)
+                add_base(G, 3, k)
+                store_rows(G, 1, k)
+            round_result(G, 1, 0, CHUNK)
+            if G == 0:
+                round_result(G, 1, CHUNK, HALF)
+
+        last = HALF - P
+        quantize_result(0, 0, 0, HALF)
+        store_words(0, 0)
+        round_result(1, 1, last, HALF, nc.vector.tensor_copy)
+        round_result(1, 1, CHUNK, last)
+        for G, h in ((1, 0), (0, 1)):
+            quantize_result(G, h, 0, HALF)
+            store_words(G, h)
+        quantize_result(1, 1, 0, CHUNK)
+        quantize_result(1, 1, last, HALF)
+        quantize_result(1, 1, CHUNK, last)
+        store_words(1, 1)
+        for r in range(4):
+            nc.sync.dma_start(out=out_2[:, r:16:4, :].rearrange("g q f -> q g f").bitcast(I32),
+                              in_=out_s[r:P:QUADRANT, :, :].bitcast(I32))

from contextlib import ExitStack

import concourse.mybir as mybir

D, F, N = 1024, 1024, 512
FLOPS = 2 * (2 * N * N * F) + 2 * (2 * D * N * F)
ALPHA = 0.5

F32 = mybir.dt.float32
BF16 = mybir.dt.bfloat16
I32 = mybir.dt.int32
U32 = mybir.dt.uint32
U8 = mybir.dt.uint8
FP8X4 = mybir.dt.float8_e4m3fn_x4
ALU = mybir.AluOpType
ACT = mybir.ActivationFunctionType

P = 128
PACK = 4
PASS = P * PACK
QUADRANT = 32
BANKS = 8
BANK = 512
CHUNK = 256
HALF = 512
COS, SIN = 0, 1
SIGN = (1.0, -1.0)
SCALE_ROW = {"coef": 0, "vc": 4, "vs": 8, "uc": 12, "us": 4}


def tile_fourierftgivenbases_x2_kernel(tc, w0, coef_words, coef_scales, g, uc_words, uc_scales,
                                                  us_words, us_scales, vc_words, vc_scales, vs_words, vs_scales,
                                                  out_0, out_1, out_2):
    nc = tc.nc
    chunks, groups, halves = F // CHUNK, D // PASS, F // HALF

    with ExitStack() as ctx:
        keep = ctx.enter_context(tc.tile_pool(name="keep", bufs=1))
        psum = ctx.enter_context(tc.psum_pool(name="psum", bufs=1))
        ctx.enter_context(tc.manual_schedule())

        def sbuf(name, shape, dtype):
            return keep.tile(shape, dtype, name=name, align_bytes=256)

        coef_raw_s = sbuf("coef_raw_s", [P, N], U8)
        vc_s = sbuf("vc_s", [P, F], U8)
        vs_u_s = sbuf("vs_u_s", [P, F + D], U8)
        raw_s = {"coef": coef_raw_s[:], "vc": vc_s[:], "vs": vs_u_s[:, :F], "uc": vs_u_s[:, F:], "us": vs_u_s[:, F:]}
        hbm_s = {"coef": coef_scales, "vc": vc_scales, "vs": vs_scales, "uc": uc_scales, "us": us_scales}
        coef_raw_w = sbuf("coef_raw_w", [P, N], U32)
        coef_w = sbuf("coef_w", [P, N], U32)
        coef_s = sbuf("coef_s", [P, N], U8)
        u_raw_w = [sbuf("u_raw_w%d" % b, [P, D], U32) for b in (COS, SIN)]
        u_w = [sbuf("u_w%d" % b, [P, D], U32) for b in (COS, SIN)]
        u_s = sbuf("u_s", [P, D], U8)
        v_w = [sbuf("v_w%d" % b, [P, F], U32) for b in (COS, SIN)]
        v_s = [raw_s[name][SCALE_ROW[name]:, :] for name in ("vc", "vs")]
        u_s_rows = [u_s[SCALE_ROW[name]:, :] for name in ("uc", "us")]
        gain_bf = sbuf("gain_bf", [P, PACK], BF16)
        gain = sbuf("gain", [P, 2, PACK], F32)
        base = [sbuf("base%d" % G, [P, PACK, F], BF16) for G in range(groups)]
        z_rows = {key: sbuf("z_rows%d_%d" % key, [P, PACK, CHUNK], BF16) for key in ((1, COS), (2, COS), (3, COS), (3, SIN))}
        z_side = [sbuf("z_side%d" % j, [P, 2, CHUNK, PACK], BF16) for j in range(chunks)]
        z_w = sbuf("z_w", [P, chunks, 2, CHUNK], U32)
        z_s = sbuf("z_s", [P, chunks, 2, CHUNK], U8)
        res = {(G, h): sbuf("res%d_%d" % (G, h), [P, PACK, HALF], F32) for h in range(halves) for G in range(groups)}
        res_side = {(G, h): sbuf("res_side%d_%d" % (G, h), [P, HALF, PACK], BF16)
                    for h in range(halves) for G in range(groups)}
        out_w = sbuf("out_w", [P, groups, F], U32)
        out_s = sbuf("out_s", [P, groups, F], U8)

        banks = {}

        def next_bank(key):
            banks[key] = psum.tile([P, BANK], F32, name="bank%d" % (len(banks) % BANKS))
            return banks[key]

        def places(t, group=0):
            return slice(PASS * group + P * t, PASS * group + P * (t + 1))

        def row_view(hbm, G):
            return hbm[PASS * G:PASS * (G + 1), :].rearrange("(p t) f -> p t f", t=PACK)

        def load_words(dst, hbm, c0, c1):
            nc.sync.dma_start(out=dst[:, c0:c1].bitcast(I32),
                              in_=hbm[0].rearrange("p n t -> p (n t)")[:, PACK * c0:PACK * c1].bitcast(I32))

        def load_scales(name, rows, queue=nc.sync):
            for r in rows:
                queue.dma_start(out=raw_s[name][SCALE_ROW[name] + r:P:QUADRANT, :].bitcast(I32),
                                in_=hbm_s[name][0, r:16:4, :].bitcast(I32))

        def load_base(G, k):
            nc.sync.dma_start(out=base[G][:, 2 * k:2 * k + 2, :], in_=row_view(w0, G)[:, 2 * k:2 * k + 2, :])

        def reorder_words(dst, src):
            nc.vector.tensor_copy(out=dst[:].bitcast(I32).rearrange("p (g t m) -> p g m t", t=PACK, m=P),
                                  in_=src[:].bitcast(I32).rearrange("p (g m t) -> p g m t", t=PACK, m=P))

        def reorder_scales(dst, src):
            nc.vector.tensor_copy(out=dst[:].rearrange("p (g t m) -> p g t m", t=PACK, m=P),
                                  in_=src.rearrange("p (g m t) -> p g t m", t=PACK, m=P))

        def z_matmul(out, t, b, c0, c1):
            nc.tensor.matmul_mx(out=out, lhsT=coef_w[:, places(t)].bitcast(FP8X4), lhsT_scale=coef_s[:, places(t)],
                                rhs=v_w[b][:, c0:c1].bitcast(FP8X4), rhs_scale=v_s[b][:, c0:c1], start=True, stop=True)

        def z_bank(j, b, k):
            bank = next_bank(("z", j, b, k))
            if (j, b) in z_rows:
                for i in range(2):
                    z_matmul(bank[:, i * CHUNK:(i + 1) * CHUNK], 2 * k + i, b, j * CHUNK, (j + 1) * CHUNK)
            else:
                for t in range(PACK):
                    z_matmul(bank[:, places(t)], t, b, j * CHUNK + k * P, j * CHUNK + (k + 1) * P)

        def z_out(j, b, k):
            bank = banks[("z", j, b, k)]
            if (j, b) in z_rows:
                for i in range(2):
                    t = 2 * k + i
                    nc.scalar.activation(out=z_rows[(j, b)][:, t, :], in_=bank[:, i * CHUNK:(i + 1) * CHUNK],
                                         func=ACT.Copy, scale=gain[:, b, t:t + 1])
            else:
                nc.vector.scalar_tensor_tensor(
                    out=z_side[j][:, b, k * P:(k + 1) * P, :], in0=bank[:].rearrange("p (t n) -> p n t", t=PACK),
                    scalar=SIGN[b], in1=gain_bf[:].unsqueeze(1).broadcast_to([P, P, PACK]), op0=ALU.mult, op1=ALU.mult)

        def z_interleave(j, b):
            nc.scalar.copy(out=z_side[j][:, b].rearrange("p (c i) t -> p c t i", i=4),
                           in_=z_rows[(j, b)][:].rearrange("p t (c i) -> p c t i", i=4))

        def z_quantize(j, first, count=1):
            bases = slice(first, first + count)
            nc.vector.quantize_mx(out=z_w[:, j, bases, :].rearrange("p b n -> p (b n)").bitcast(FP8X4),
                                  scales=z_s[:, j, bases, :].rearrange("p b n -> p (b n)"),
                                  in_=z_side[j][:, bases].rearrange("p b n t -> p (b n t)"))

        def out_bank(G, j, k):
            bank = next_bank(("out", G, j, k))
            for i in range(2):
                cols = places(2 * k + i, G)
                for b in (COS, SIN):
                    nc.tensor.matmul_mx(out=bank[:, i * CHUNK:(i + 1) * CHUNK],
                                        lhsT=u_w[b][:, cols].bitcast(FP8X4), lhsT_scale=u_s_rows[b][:, cols],
                                        rhs=z_w[:, j, b, :].bitcast(FP8X4), rhs_scale=z_s[:, j, b, :],
                                        start=(b == COS), stop=(b == SIN))

        def add_base(G, j, k):
            h, c0 = divmod(j * CHUNK, HALF)
            nc.vector.scalar_tensor_tensor(
                out=res[(G, h)][:, 2 * k:2 * k + 2, c0:c0 + CHUNK],
                in0=banks[("out", G, j, k)][:].rearrange("p (t n) -> p t n", t=2), scalar=ALPHA,
                in1=base[G][:, 2 * k:2 * k + 2, j * CHUNK:(j + 1) * CHUNK], op0=ALU.mult, op1=ALU.add)

        def store_rows(G, h, k):
            nc.sync.dma_start(out=row_view(out_0, G)[:, 2 * k:2 * k + 2, h * HALF:(h + 1) * HALF],
                              in_=res[(G, h)][:, 2 * k:2 * k + 2, :])

        def round_result(G, h, c0, c1, copy=nc.scalar.copy):
            copy(out=res_side[(G, h)][:, c0:c1, :].rearrange("p (c i) t -> p c t i", i=2),
                 in_=res[(G, h)][:, :, c0:c1].rearrange("p t (c i) -> p c t i", i=2))

        def quantize_result(G, h, c0, c1):
            cols = slice(h * HALF + c0, h * HALF + c1)
            nc.vector.quantize_mx(out=out_w[:, G, cols].bitcast(FP8X4), scales=out_s[:, G, cols],
                                  in_=res_side[(G, h)][:, c0:c1, :].rearrange("p n t -> p (n t)"))

        def store_words(G, h):
            nc.sync.dma_start(
                out=out_1[G].rearrange("p f t -> p (f t)")[:, PACK * HALF * h:PACK * HALF * (h + 1)].bitcast(I32),
                in_=out_w[:, G, h * HALF:(h + 1) * HALF].bitcast(I32))

        nc.gpsimd.memset(vc_s[:].bitcast(I32), 0)
        nc.vector.memset(coef_raw_s[:].bitcast(I32), 0)
        nc.vector.memset(vs_u_s[:].bitcast(I32), 0)

        nc.gpsimd.dma_start(out=gain_bf[:], in_=g.rearrange("(p t) -> p t", t=PACK))
        load_scales("us", (2, 3), nc.gpsimd)
        load_words(coef_raw_w, coef_words, 0, N)
        load_scales("coef", range(4))
        load_scales("vc", (0,))
        load_words(v_w[COS], vc_words, 0, HALF)
        load_words(u_raw_w[SIN], us_words, 0, D)
        load_scales("vc", (1, 2, 3))
        load_words(v_w[SIN], vs_words, 0, HALF)
        load_scales("vs", (0, 1))
        load_words(u_raw_w[COS], uc_words, 0, D)
        load_scales("vs", (2, 3))
        load_scales("uc", (0,))
        load_words(v_w[COS], vc_words, HALF, F)
        load_scales("uc", (1, 2))
        load_base(0, 0)
        load_scales("uc", (3,))
        load_scales("us", (0, 1))
        load_words(v_w[SIN], vs_words, HALF, F)
        load_base(0, 1)
        load_base(1, 0)
        load_base(1, 1)

        for b in (COS, SIN):
            nc.scalar.activation(out=gain[:, b, :], in_=gain_bf[:], func=ACT.Copy, scale=SIGN[b])
        reorder_words(coef_w, coef_raw_w)
        reorder_scales(coef_s, raw_s["coef"])
        reorder_words(u_w[SIN], u_raw_w[SIN])

        for j, b in ((0, COS), (1, COS), (0, SIN), (2, COS)):
            for k in range(2):
                z_bank(j, b, k)
        for j in (0, 1):
            for k in range(2):
                z_out(j, COS, k)
        reorder_words(u_w[COS], u_raw_w[COS])
        z_quantize(0, COS)
        for j, b in ((1, SIN), (3, COS)):
            for k in range(2):
                z_bank(j, b, k)
        for j, b in ((0, SIN), (2, COS)):
            for k in range(2):
                z_out(j, b, k)
        z_interleave(1, COS)
        for j, k in ((2, 0), (3, 0), (3, 1), (2, 1)):
            z_bank(j, SIN, k)
        reorder_scales(u_s, raw_s["uc"])
        z_quantize(0, SIN)
        for k in range(2):
            z_out(1, SIN, k)
            out_bank(0, 0, k)
        for b in (COS, SIN):
            for k in range(2):
                z_out(3, b, k)
        z_out(2, SIN, 0)
        z_quantize(1, COS)
        z_quantize(1, SIN)
        for j, b in ((2, COS), (3, COS), (3, SIN)):
            z_interleave(j, b)

        for k in range(2):
            out_bank(0, 1, k)
        add_base(0, 0, 0)
        z_out(2, SIN, 1)
        for k in range(2):
            out_bank(1, 0, k)
            out_bank(1, 1, k)
        add_base(0, 1, 0)
        store_rows(0, 0, 0)
        add_base(0, 0, 1)
        z_quantize(2, COS, 2)
        add_base(0, 1, 1)
        store_rows(0, 0, 1)
        for c0 in (0, CHUNK):
            round_result(0, 0, c0, c0 + CHUNK)
        out_bank(0, 2, 0)
        add_base(1, 0, 0)
        add_base(1, 1, 0)
        store_rows(1, 0, 0)
        z_quantize(3, COS, 2)
        out_bank(0, 3, 0)
        out_bank(0, 2, 1)
        out_bank(0, 3, 1)
        add_base(1, 0, 1)
        add_base(1, 1, 1)
        store_rows(1, 0, 1)
        for c0 in (0, CHUNK):
            round_result(1, 0, c0, c0 + CHUNK)
        for k in range(2):
            out_bank(1, 2, k)
            out_bank(1, 3, k)

        for G in range(groups):
            for k in range(2):
                add_base(G, 2, k)
                add_base(G, 3, k)
                store_rows(G, 1, k)
            round_result(G, 1, 0, CHUNK)
            if G == 0:
                round_result(G, 1, CHUNK, HALF)

        last = HALF - P
        quantize_result(0, 0, 0, HALF)
        store_words(0, 0)
        round_result(1, 1, last, HALF, nc.vector.tensor_copy)
        round_result(1, 1, CHUNK, last)
        for G, h in ((1, 0), (0, 1)):
            quantize_result(G, h, 0, HALF)
            store_words(G, h)
        quantize_result(1, 1, 0, CHUNK)
        quantize_result(1, 1, last, HALF)
        quantize_result(1, 1, CHUNK, last)
        store_words(1, 1)
        for r in range(4):
            nc.sync.dma_start(out=out_2[:, r:16:4, :].rearrange("g q f -> q g f").bitcast(I32),
                              in_=out_s[r:P:QUADRANT, :, :].bitcast(I32))
